import numpy as np
import ml_dtypes


def mxq(x, axis, fmt="e4m3"):
    dtype, down = {"e4m3": (ml_dtypes.float8_e4m3fn, 7), "e5m2": (ml_dtypes.float8_e5m2, 14)}[fmt]
    v = np.moveaxis(np.asarray(x, np.float32).astype(ml_dtypes.bfloat16).astype(np.float64), axis, -1)
    blocks = v.reshape(v.shape[:-1] + (-1, 32))
    amax = np.abs(blocks).max(-1, keepdims=True)
    byte = np.maximum(np.where(amax > 0, np.frexp(amax)[1] - 1 + 127, 0) - down, 1)
    scale = np.exp2(byte - 127.0)
    codes = (blocks / scale).astype(np.float32).astype(dtype).astype(np.float64)
    return np.moveaxis((codes * scale).reshape(v.shape), -1, axis)


WIDE = False


def mx_kscale(k):
    if not WIDE:
        return np.ones(k)
    levels = np.array([10, -10, 5, -5, 0])
    if k % 512:
        return np.exp2(np.random.permutation(np.resize(levels, k // 32))).repeat(32)
    a = np.empty((k // 512, 16))
    for p in range(k // 512):
        a[p, :8] = np.random.permutation(np.resize(levels, 8))
        for g in range(8):
            far = levels[np.abs(levels - a[p, g]) >= 10]
            a[p, g + 8] = far[np.random.randint(len(far))]
    return np.exp2(a.ravel()).repeat(32)


def f64(x):
    return np.asarray(x).astype(np.float64)


def striped(idx):
    return np.tile(idx.reshape(-1, 16).T, (8, 1)).astype(np.uint16)


def unstriped(offs):
    return offs[:16].T.reshape(-1).astype(np.int64)


def striped8(idx):
    return np.concatenate([x.reshape(-1, 16).T for x in idx]).astype(np.uint16)


def runs(offs, k):
    lists = np.stack([offs[16 * r : 16 * r + 16].T.reshape(-1) for r in range(8)]).astype(np.int64)
    return lists[np.arange(k) % 512 // 64]


def pack_weight(w):
    k, n = w.shape
    w = f64(np.asarray(w, np.float32).astype(ml_dtypes.bfloat16)).reshape(k // 32, 32, n)
    amax = np.abs(w).max(1)
    byte = np.clip(np.where(amax > 0, np.frexp(amax)[1] - 1 + 127 - 7, 1), 1, 254)
    scaled = (w * np.exp2(127.0 - byte)[:, None, :]).reshape(k, n).astype(np.float32)
    words = np.ascontiguousarray(scaled.reshape(k // 512, 128, 4, n).transpose(0, 1, 3, 2)).astype(ml_dtypes.float8_e4m3fn).view(np.uint8)
    return words, np.ascontiguousarray(byte.astype(np.uint8).reshape(k // 512, 16, n))


def unpack_weight(words, scales):
    g, p, n, _ = words.shape
    vals = np.ascontiguousarray(words).view(ml_dtypes.float8_e4m3fn).astype(np.float64) * np.repeat(np.exp2(scales.astype(np.float64) - 127.0), 8, axis=1)[..., None]
    return vals.transpose(0, 1, 3, 2).reshape(g * 512, n)


K, T, S, N = 512, 2048, 512, 512


def setup_inputs():
    n = np.random.standard_normal
    s = mx_kscale(K)[:, None]
    packed_xT = pack_weight(n((K, T)) * s)
    return {
        "x_words": packed_xT[0],
        "x_scales": packed_xT[1],
        "w1": (n((K, N)) / np.sqrt(K) / s).astype(np.float32),
        "offs": striped(np.random.permutation(T)[:S]),
        "n1": striped8(np.stack([np.random.permutation(S) for _ in range(8)])),
        "n2": striped8(np.stack([np.random.permutation(S) for _ in range(8)])),
        "n3": striped8(np.stack([np.random.permutation(S) for _ in range(8)])),
    }


def reference(x_words, x_scales, w1, offs, n1, n2, n3):
    xq = unpack_weight(x_words, x_scales)[:, unstriped(offs)]
    y = mxq(f64(w1), 0, "e4m3").T @ xq
    e0 = np.exp(y)
    return np.log(e0 + e0[np.arange(N)[:, None], runs(n1, N)] + e0[np.arange(N)[:, None], runs(n2, N)] + e0[np.arange(N)[:, None], runs(n3, N)]) - y

@@ -1,0 +1,182 @@
+from contextlib import ExitStack
+
+import concourse.mybir as mybir
+from concourse.masks import make_identity
+
+K, T, S, N = 512, 2048, 512, 512
+FLOPS = 2 * K * N * S
+
+F32 = mybir.dt.float32
+BF16 = mybir.dt.bfloat16
+I32 = mybir.dt.int32
+U32 = mybir.dt.uint32
+U16 = mybir.dt.uint16
+U8 = mybir.dt.uint8
+FP8X4 = mybir.dt.float8_e4m3fn_x4
+EXP = mybir.ActivationFunctionType.Exp
+LN = mybir.ActivationFunctionType.Ln
+ADD = mybir.AluOpType.add
+SUB = mybir.AluOpType.subtract
+
+P = 128
+HALF = S // 2
+HALVES = [slice(0, HALF), slice(HALF, S)]
+LIST_HALVES = [slice(0, HALF // 16), slice(HALF // 16, S // 16)]
+M_SPLIT = 80
+
+
+def tile_picked_nce8_none_p_kernel(tc, x_words, x_scales, w1, offs, n1, n2, n3, out):
+    nc = tc.nc
+    with ExitStack() as ctx:
+        keep = ctx.enter_context(tc.tile_pool(name="keep", bufs=1))
+        psum = ctx.enter_context(tc.psum_pool(name="psum", bufs=1))
+
+        def sb(name, dtype=F32, width=S):
+            return keep.tile([P, width], dtype, name=name, align_bytes=64)
+
+        def bank(number, name, width):
+            return psum.tile([P, width], F32, name=name, tag="bank%d" % number)
+
+        key_scales = sb("key_scales", U8, T)
+        nc.vector.memset(key_scales[:].bitcast(I32), 0)
+
+        offs_sb = keep.tile([P, S // 16], U16, name="offs_sb")
+        nc.sync.dma_start(offs_sb[:], offs)
+        w_raw = keep.tile([P, 4, N], F32, name="w_raw")
+        w_rows = w1.rearrange("(p j) c -> p j c", j=4)
+        nc.sync.dma_start(w_raw[:, 0:2, :], w_rows[:, 0:2, :])
+        for q in range(4):
+            nc.sync.dma_start(key_scales[32 * q : 32 * q + 4, :].bitcast(I32), x_scales[0, 4 * q : 4 * q + 4, :].bitcast(I32))
+        nc.sync.dma_start(w_raw[:, 2:4, :], w_rows[:, 2:4, :])
+        key_words = sb("key_words", U32, T)
+        nc.sync.dma_start(key_words[:].bitcast(I32), x_words[0].rearrange("p c r -> p (c r)").bitcast(I32))
+        lists = []
+        for name, source in (("n1_sb", n1), ("n2_sb", n2), ("n3_sb", n3)):
+            list_sb = keep.tile([P, S // 16], U16, name=name)
+            nc.sync.dma_start(list_sb[:], source)
+            lists.append(list_sb)
+
+        warm_in = sb("warm_in", F32, 1)
+        warm_out = sb("warm_out", F32, 1)
+        nc.vector.memset(warm_in[:], 0.0)
+        nc.scalar.activation(warm_out[:], warm_in[:], EXP)
+
+        identity = sb("identity", F32, P)
+        make_identity(nc, identity[:])
+
+        picked_scales = sb("picked_scales", U8)
+        nc.vector.tensor_copy(picked_scales[:], key_scales[:].indirect(offs_sb[:]))
+
+        w_grouped = sb("w_grouped", BF16, 4 * N)
+        grouped_view = w_grouped[:].rearrange("p (t m j) -> p m j t", t=4, j=4)
+        raw_view = w_raw[:].rearrange("p j (m t) -> p m j t", t=4)
+        nc.vector.tensor_copy(grouped_view[:, :M_SPLIT], raw_view[:, :M_SPLIT])
+        nc.scalar.copy(grouped_view[:, M_SPLIT:], raw_view[:, M_SPLIT:])
+        w_codes = sb("w_codes", U32, N)
+        w_scales = sb("w_scales", U8, N)
+        nc.vector.quantize_mx(out=w_codes[:].bitcast(FP8X4), scales=w_scales[:], in_=w_grouped[:])
+
+        picked_words = sb("picked_words", U32)
+        for h in range(2):
+            nc.vector.tensor_copy(picked_words[:, HALVES[h]], key_words[:].indirect(offs_sb[:, LIST_HALVES[h]]))
+
+        def product(t, cols, acc):
+            rows = slice(P * t, P * (t + 1))
+            nc.tensor.matmul_mx(
+                out=acc[:],
+                lhsT=w_codes[:, rows].bitcast(FP8X4),
+                lhsT_scale=w_scales[:, rows],
+                rhs=picked_words[:, cols].bitcast(FP8X4),
+                rhs_scale=picked_scales[:, cols],
+                start=True,
+                stop=True,
+            )
+
+        A, B, C, D = 0, 1, 2, 3
+        y_half = {}
+        for h in range(2):
+            for number, t in enumerate((A, D)):
+                y_half[t, h] = bank(2 * h + number, "y_half_%d_%d" % (t, h), HALF)
+                product(t, HALVES[h], y_half[t, h])
+        y_bank = {}
+        for number, t in enumerate((B, C)):
+            y_bank[t] = bank(4 + number, "y_bank_%d" % t, S)
+            product(t, slice(0, S), y_bank[t])
+
+        e0 = [sb("e0_%d" % t) for t in range(4)]
+        y_sb = {t: sb("y_%d" % t) for t in (A, D)}
+        for h in range(2):
+            nc.scalar.activation(e0[A][:, HALVES[h]], y_half[A, h][:], EXP)
+            nc.vector.tensor_copy(y_sb[D][:, HALVES[h]], y_half[D, h][:])
+            nc.vector.tensor_copy(y_sb[A][:, HALVES[h]], y_half[A, h][:])
+
+        def scalar_lookup(t, i):
+            got = sb("got_%d_%d" % (t, i))
+            for h in range(2):
+                nc.scalar.activation(got[:, HALVES[h]], y_sb[t][:].indirect(lists[i][:, LIST_HALVES[h]]), EXP)
+            return got
+
+        def vector_lookups(t, numbers, total):
+            for i in numbers:
+                grown = sb("sum_%d_%d" % (t, i))
+                for h in range(2):
+                    looked_up = e0[t][:].indirect(lists[i][:, LIST_HALVES[h]])
+                    if total is None:
+                        nc.vector.tensor_copy(grown[:, HALVES[h]], looked_up)
+                    else:
+                        nc.vector.tensor_tensor(grown[:, HALVES[h]], looked_up, total[:, HALVES[h]], ADD)
+                total = grown
+            return total
+
+        def exp_twice(t):
+            again = sb("e0_again_%d" % t)
+            nc.scalar.activation(e0[t][:], y_bank[t][:], EXP)
+            nc.scalar.activation(again[:], y_bank[t][:], EXP)
+            return again
+
+        def sum_turned(terms, number, name):
+            turned = bank(number, name, S)
+            for b in range(4):
+                cols = slice(P * b, P * (b + 1))
+                for n, term in enumerate(terms):
+                    nc.tensor.matmul(turned[:, cols], term[:, cols], identity[:], is_transpose=True, start=(n == 0), stop=(n == len(terms) - 1))
+            return turned
+
+        out_rows = out.rearrange("(p t) j -> p t j", t=4)
+
+        def finish_turned(t, turned, number):
+            log_turned = sb("log_turned_%d" % t)
+            nc.scalar.activation(log_turned[:], turned[:], LN)
+            log_bank = bank(number, "log_bank_%d" % t, S)
+            for b in range(4):
+                cols = slice(P * b, P * (b + 1))
+                nc.tensor.transpose(log_bank[:, cols], log_turned[:, cols], identity[:])
+            loss = sb("loss_%d" % t)
+            nc.vector.tensor_tensor(loss[:], log_bank[:], y_sb[t][:], SUB)
+            nc.sync.dma_start(out_rows[:, t, :], loss[:])
+
+        def finish(t, total, pieces):
+            log_sum = sb("log_sum_%d" % t)
+            loss = sb("loss_%d" % t)
+            for cols in pieces:
+                nc.scalar.activation(log_sum[:, cols], total[:, cols], LN)
+                nc.vector.tensor_tensor(loss[:, cols], log_sum[:, cols], y_bank[t][:, cols], SUB)
+                nc.sync.dma_start(out_rows[:, t, cols], loss[:, cols])
+
+        pair_a = vector_lookups(A, (1, 2), None)
+        got_d0 = scalar_lookup(D, 0)
+        again_b = exp_twice(B)
+        sum_b = vector_lookups(B, (0, 1, 2), again_b)
+        got_a0 = scalar_lookup(A, 0)
+        turned_a = sum_turned([e0[A], got_a0, pair_a], 6, "turned_a")
+        got_d1 = scalar_lookup(D, 1)
+        again_c = exp_twice(C)
+        sum_c = vector_lookups(C, (0, 1, 2), again_c)
+        nc.scalar.activation(e0[D][:], y_sb[D][:], EXP)
+        got_d2 = scalar_lookup(D, 2)
+        turned_d = sum_turned([e0[D], got_d0, got_d1, got_d2], 7, "turned_d")
+
+        finish_turned(A, turned_a, 0)
+        finish(B, sum_b, [slice(0, S)])
+        finish_turned(D, turned_d, 1)
+        finish(C, sum_c, HALVES)

@@ -13,16 +13,24 @@ U32 = mybir.dt.uint32
 U16 = mybir.dt.uint16
 U8 = mybir.dt.uint8
 FP8X4 = mybir.dt.float8_e4m3fn_x4
+COPY = mybir.ActivationFunctionType.Copy
 EXP = mybir.ActivationFunctionType.Exp
 LN = mybir.ActivationFunctionType.Ln
 ADD = mybir.AluOpType.add
 SUB = mybir.AluOpType.subtract
 
 P = 128
-HALF = S // 2
-HALVES = [slice(0, HALF), slice(HALF, S)]
-LIST_HALVES = [slice(0, HALF // 16), slice(HALF // 16, S // 16)]
-M_SPLIT = 80
+PACK = 4
+TILES = N // P
+PER_LIST_COLUMN = 16
+SHARED, EARLY, LATE, SCALARS = 0, 1, 2, 3
+
+WHOLE = slice(0, S)
+HALVES = [slice(0, S // 2), slice(S // 2, S)]
+LAST_QUARTERS = [slice(S // 2, S // 2 + P), slice(S // 2 + P, S)]
+WINDOW = 2 * S
+VECTOR_ROWS = 96
+W_LOADS = [slice(0, PACK // 2), slice(PACK // 2, PACK)]
 
 
 def tile_picked_nce8_none_p_kernel(tc, x_words, x_scales, w1, offs, n1, n2, n3, out):
@@ -31,59 +39,69 @@ def tile_picked_nce8_none_p_kernel(tc, x_words, x_scales, w1, offs, n1, n2, n3, 
         keep = ctx.enter_context(tc.tile_pool(name="keep", bufs=1))
         psum = ctx.enter_context(tc.psum_pool(name="psum", bufs=1))
 
-        def sb(name, dtype=F32, width=S):
-            return keep.tile([P, width], dtype, name=name, align_bytes=64)
+        def sbuf(name, dtype=F32, width=S, tag=None):
+            return keep.tile([P, width], dtype, name=name, tag=tag or name, align_bytes=64)
 
         def bank(number, name, width):
             return psum.tile([P, width], F32, name=name, tag="bank%d" % number)
 
-        key_scales = sb("key_scales", U8, T)
+        def entries(list_tile, cols):
+            return list_tile[:, cols.start // PER_LIST_COLUMN : cols.stop // PER_LIST_COLUMN]
+
+        key_scales = sbuf("key_scales", U8, T)
         nc.vector.memset(key_scales[:].bitcast(I32), 0)
 
-        offs_sb = keep.tile([P, S // 16], U16, name="offs_sb")
+        w_raw = keep.tile([P, PACK, N], F32, name="w_raw")
+        w_rows = w1.rearrange("(p r) c -> p r c", r=PACK)
+        nc.sync.dma_start(w_raw[:, W_LOADS[0], :], w_rows[:, W_LOADS[0], :])
+        offs_sb = keep.tile([P, S // PER_LIST_COLUMN], U16, name="offs_sb")
         nc.sync.dma_start(offs_sb[:], offs)
-        w_raw = keep.tile([P, 4, N], F32, name="w_raw")
-        w_rows = w1.rearrange("(p j) c -> p j c", j=4)
-        nc.sync.dma_start(w_raw[:, 0:2, :], w_rows[:, 0:2, :])
         for q in range(4):
             nc.sync.dma_start(key_scales[32 * q : 32 * q + 4, :].bitcast(I32), x_scales[0, 4 * q : 4 * q + 4, :].bitcast(I32))
-        nc.sync.dma_start(w_raw[:, 2:4, :], w_rows[:, 2:4, :])
-        key_words = sb("key_words", U32, T)
+        nc.sync.dma_start(w_raw[:, W_LOADS[1], :], w_rows[:, W_LOADS[1], :])
+        key_words = sbuf("key_words", U32, T)
         nc.sync.dma_start(key_words[:].bitcast(I32), x_words[0].rearrange("p c r -> p (c r)").bitcast(I32))
-        lists = []
+        negatives = []
         for name, source in (("n1_sb", n1), ("n2_sb", n2), ("n3_sb", n3)):
-            list_sb = keep.tile([P, S // 16], U16, name=name)
+            list_sb = keep.tile([P, S // PER_LIST_COLUMN], U16, name=name)
             nc.sync.dma_start(list_sb[:], source)
-            lists.append(list_sb)
+            negatives.append(list_sb)
 
-        warm_in = sb("warm_in", F32, 1)
-        warm_out = sb("warm_out", F32, 1)
-        nc.vector.memset(warm_in[:], 0.0)
-        nc.scalar.activation(warm_out[:], warm_in[:], EXP)
-
-        identity = sb("identity", F32, P)
+        identity = sbuf("identity", F32, P)
         make_identity(nc, identity[:])
 
-        picked_scales = sb("picked_scales", U8)
+        picked_scales = sbuf("picked_scales", U8)
         nc.vector.tensor_copy(picked_scales[:], key_scales[:].indirect(offs_sb[:]))
 
-        w_grouped = sb("w_grouped", BF16, 4 * N)
-        grouped_view = w_grouped[:].rearrange("p (t m j) -> p m j t", t=4, j=4)
-        raw_view = w_raw[:].rearrange("p j (m t) -> p m j t", t=4)
-        nc.vector.tensor_copy(grouped_view[:, :M_SPLIT], raw_view[:, :M_SPLIT])
-        nc.scalar.copy(grouped_view[:, M_SPLIT:], raw_view[:, M_SPLIT:])
-        w_codes = sb("w_codes", U32, N)
-        w_scales = sb("w_scales", U8, N)
+        w_grouped = sbuf("w_grouped", BF16, PACK * N)
+        grouped_view = w_grouped[:].rearrange("p (t m r) -> p m r t", t=TILES, r=PACK)
+        raw_view = w_raw[:].rearrange("p r (m t) -> p m r t", t=TILES)
+        nc.vector.tensor_copy(grouped_view[:, :VECTOR_ROWS], raw_view[:, :VECTOR_ROWS])
+        for planes in W_LOADS:
+            nc.scalar.activation(grouped_view[:, VECTOR_ROWS:, planes], raw_view[:, VECTOR_ROWS:, planes], COPY)
+        w_codes = sbuf("w_codes", U32, N)
+        w_scales = sbuf("w_scales", U8, N)
         nc.vector.quantize_mx(out=w_codes[:].bitcast(FP8X4), scales=w_scales[:], in_=w_grouped[:])
 
-        picked_words = sb("picked_words", U32)
-        for h in range(2):
-            nc.vector.tensor_copy(picked_words[:, HALVES[h]], key_words[:].indirect(offs_sb[:, LIST_HALVES[h]]))
+        picked_words = sbuf("picked_words", U32)
+        for cols in HALVES:
+            nc.vector.tensor_copy(picked_words[:, cols], key_words[:].indirect(entries(offs_sb, cols)))
 
-        def product(t, cols, acc):
+        pieces = [
+            (SHARED, HALVES[0]),
+            (EARLY, HALVES[0]),
+            (SHARED, LAST_QUARTERS[0]),
+            (SHARED, LAST_QUARTERS[1]),
+            (EARLY, HALVES[1]),
+            (LATE, WHOLE),
+            (SCALARS, WHOLE),
+        ]
+        y_psum = {t: [] for t in range(TILES)}
+        for number, (t, cols) in enumerate(pieces):
             rows = slice(P * t, P * (t + 1))
+            scores = bank(number, "y_piece_%d" % number, cols.stop - cols.start)
             nc.tensor.matmul_mx(
-                out=acc[:],
+                out=scores[:],
                 lhsT=w_codes[:, rows].bitcast(FP8X4),
                 lhsT_scale=w_scales[:, rows],
                 rhs=picked_words[:, cols].bitcast(FP8X4),
@@ -91,92 +109,98 @@ def tile_picked_nce8_none_p_kernel(tc, x_words, x_scales, w1, offs, n1, n2, n3, 
                 start=True,
                 stop=True,
             )
+            y_psum[t].append(scores)
 
-        A, B, C, D = 0, 1, 2, 3
-        y_half = {}
-        for h in range(2):
-            for number, t in enumerate((A, D)):
-                y_half[t, h] = bank(2 * h + number, "y_half_%d_%d" % (t, h), HALF)
-                product(t, HALVES[h], y_half[t, h])
-        y_bank = {}
-        for number, t in enumerate((B, C)):
-            y_bank[t] = bank(4 + number, "y_bank_%d" % t, S)
-            product(t, slice(0, S), y_bank[t])
+        e0 = [sbuf("e0_%d" % t, F32, S if t == SCALARS else WINDOW) for t in range(TILES)]
+        y_sb = {t: sbuf("y_%d" % t, F32, WINDOW) for t in (SHARED, SCALARS)}
+        e0_copy = {t: sbuf("e0_copy_%d" % t) for t in (EARLY, LATE)}
 
-        e0 = [sb("e0_%d" % t) for t in range(4)]
-        y_sb = {t: sb("y_%d" % t) for t in (A, D)}
-        for h in range(2):
-            nc.scalar.activation(e0[A][:, HALVES[h]], y_half[A, h][:], EXP)
-            nc.vector.tensor_copy(y_sb[D][:, HALVES[h]], y_half[D, h][:])
-            nc.vector.tensor_copy(y_sb[A][:, HALVES[h]], y_half[A, h][:])
+        def shared_piece(piece, cols):
+            nc.scalar.activation(e0[SHARED][:, cols], y_psum[SHARED][piece][:], EXP)
+            nc.vector.tensor_copy(y_sb[SHARED][:, cols], y_psum[SHARED][piece][:])
 
-        def scalar_lookup(t, i):
-            got = sb("got_%d_%d" % (t, i))
-            for h in range(2):
-                nc.scalar.activation(got[:, HALVES[h]], y_sb[t][:].indirect(lists[i][:, LIST_HALVES[h]]), EXP)
-            return got
+        shared_piece(0, HALVES[0])
+        nc.scalar.activation(e0[EARLY][:, HALVES[0]], y_psum[EARLY][0][:], EXP)
+        nc.vector.tensor_copy(e0_copy[EARLY][:, HALVES[0]], e0[EARLY][:, HALVES[0]])
+        shared_piece(1, LAST_QUARTERS[0])
+        shared_piece(2, LAST_QUARTERS[1])
+        nc.scalar.activation(e0[EARLY][:, HALVES[1]], y_psum[EARLY][1][:], EXP)
 
-        def vector_lookups(t, numbers, total):
-            for i in numbers:
-                grown = sb("sum_%d_%d" % (t, i))
-                for h in range(2):
-                    looked_up = e0[t][:].indirect(lists[i][:, LIST_HALVES[h]])
-                    if total is None:
-                        nc.vector.tensor_copy(grown[:, HALVES[h]], looked_up)
-                    else:
-                        nc.vector.tensor_tensor(grown[:, HALVES[h]], looked_up, total[:, HALVES[h]], ADD)
-                total = grown
-            return total
+        def scalar_lookup(t, i, spans):
+            found = sbuf("found_%d_%d" % (t, i))
+            for cols in spans:
+                nc.scalar.activation(found[:, cols], y_sb[t][:].indirect(entries(negatives[i], cols)), EXP)
+            return found
 
-        def exp_twice(t):
-            again = sb("e0_again_%d" % t)
-            nc.scalar.activation(e0[t][:], y_bank[t][:], EXP)
-            nc.scalar.activation(again[:], y_bank[t][:], EXP)
-            return again
+        def vector_lookup(t, i):
+            found = sbuf("found_%d_%d" % (t, i))
+            nc.vector.tensor_copy(found[:], e0[t][:].indirect(negatives[i][:]))
+            return found
 
-        def sum_turned(terms, number, name):
+        def lookup_and_add(t, i, total, spans, tag=None):
+            grown = sbuf("sum_%d_%d" % (t, i), tag=tag)
+            for cols in spans:
+                nc.vector.tensor_tensor(grown[:, cols], e0[t][:].indirect(entries(negatives[i], cols)), total[:, cols], ADD)
+            return grown
+
+        def turned_sum(terms, number, name):
             turned = bank(number, name, S)
-            for b in range(4):
+            for b in range(S // P):
                 cols = slice(P * b, P * (b + 1))
                 for n, term in enumerate(terms):
                     nc.tensor.matmul(turned[:, cols], term[:, cols], identity[:], is_transpose=True, start=(n == 0), stop=(n == len(terms) - 1))
             return turned
 
-        out_rows = out.rearrange("(p t) j -> p t j", t=4)
+        shared_n3 = vector_lookup(SHARED, 2)
+        nc.vector.tensor_copy(e0_copy[EARLY][:, HALVES[1]], e0[EARLY][:, HALVES[1]])
+        shared_n2 = vector_lookup(SHARED, 1)
+        nc.scalar.activation(e0[LATE][:, WHOLE], y_psum[LATE][0][:], EXP)
+        nc.sync.dma_start(e0_copy[LATE][:], e0[LATE][:, WHOLE])
+        shared_n1 = scalar_lookup(SHARED, 0, [WHOLE])
+        turned_shared = turned_sum([e0[SHARED], shared_n1, shared_n2, shared_n3], 7, "turned_shared")
+        nc.scalar.copy(y_sb[SCALARS][:, WHOLE], y_psum[SCALARS][0][:])
 
-        def finish_turned(t, turned, number):
-            log_turned = sb("log_turned_%d" % t)
+        sum_early = lookup_and_add(EARLY, 0, e0_copy[EARLY], [WHOLE])
+        sum_late = lookup_and_add(LATE, 0, e0_copy[LATE], [WHOLE])
+        sum_early = lookup_and_add(EARLY, 1, sum_early, [WHOLE], tag="e0_copy_%d" % LATE)
+        sum_late = lookup_and_add(LATE, 1, sum_late, [WHOLE])
+        sum_early = lookup_and_add(EARLY, 2, sum_early, [WHOLE])
+        sum_late = lookup_and_add(LATE, 2, sum_late, HALVES)
+
+        scalars_n1 = scalar_lookup(SCALARS, 0, [WHOLE])
+        scalars_n2 = scalar_lookup(SCALARS, 1, [WHOLE])
+        nc.scalar.activation(e0[SCALARS][:], y_sb[SCALARS][:, WHOLE], EXP)
+        scalars_n3 = scalar_lookup(SCALARS, 2, HALVES)
+        turned_scalars = turned_sum([e0[SCALARS], scalars_n1, scalars_n2, scalars_n3], 0, "turned_scalars")
+
+        out_rows = out.rearrange("(p t) j -> p t j", t=TILES)
+        loss = [sbuf("loss_%d" % t) for t in range(TILES)]
+
+        def log_turned_back(t, turned, number):
+            log_turned = sbuf("log_turned_%d" % t)
             nc.scalar.activation(log_turned[:], turned[:], LN)
-            log_bank = bank(number, "log_bank_%d" % t, S)
-            for b in range(4):
+            logs = bank(number, "log_bank_%d" % t, S)
+            for b in range(S // P):
                 cols = slice(P * b, P * (b + 1))
-                nc.tensor.transpose(log_bank[:, cols], log_turned[:, cols], identity[:])
-            loss = sb("loss_%d" % t)
-            nc.vector.tensor_tensor(loss[:], log_bank[:], y_sb[t][:], SUB)
-            nc.sync.dma_start(out_rows[:, t, :], loss[:])
+                nc.tensor.transpose(logs[:, cols], log_turned[:, cols], identity[:])
+            return logs
 
-        def finish(t, total, pieces):
-            log_sum = sb("log_sum_%d" % t)
-            loss = sb("loss_%d" % t)
-            for cols in pieces:
-                nc.scalar.activation(log_sum[:, cols], total[:, cols], LN)
-                nc.vector.tensor_tensor(loss[:, cols], log_sum[:, cols], y_bank[t][:, cols], SUB)
-                nc.sync.dma_start(out_rows[:, t, cols], loss[:, cols])
+        def subtract_and_store(t, cols, logs, scores):
+            nc.vector.tensor_tensor(loss[t][:, cols], logs, scores, SUB)
+            nc.sync.dma_start(out_rows[:, t, cols], loss[t][:, cols])
 
-        pair_a = vector_lookups(A, (1, 2), None)
-        got_d0 = scalar_lookup(D, 0)
-        again_b = exp_twice(B)
-        sum_b = vector_lookups(B, (0, 1, 2), again_b)
-        got_a0 = scalar_lookup(A, 0)
-        turned_a = sum_turned([e0[A], got_a0, pair_a], 6, "turned_a")
-        got_d1 = scalar_lookup(D, 1)
-        again_c = exp_twice(C)
-        sum_c = vector_lookups(C, (0, 1, 2), again_c)
-        nc.scalar.activation(e0[D][:], y_sb[D][:], EXP)
-        got_d2 = scalar_lookup(D, 2)
-        turned_d = sum_turned([e0[D], got_d0, got_d1, got_d2], 7, "turned_d")
+        def log_subtract_store(t, cols, total, logs, scores):
+            nc.scalar.activation(logs[:, cols], total[:, cols], LN)
+            subtract_and_store(t, cols, logs[:, cols], scores)
 
-        finish_turned(A, turned_a, 0)
-        finish(B, sum_b, [slice(0, S)])
-        finish_turned(D, turned_d, 1)
-        finish(C, sum_c, HALVES)
+        log_early = sbuf("log_early", tag="found_%d_%d" % (SHARED, 0))
+        log_late = sbuf("log_late", tag="found_%d_%d" % (SCALARS, 2))
+        log_shared = log_turned_back(SHARED, turned_shared, 2)
+        log_subtract_store(EARLY, HALVES[0], sum_early, log_early, y_psum[EARLY][0][:])
+        subtract_and_store(SHARED, WHOLE, log_shared[:], y_sb[SHARED][:, WHOLE])
+        log_scalars = log_turned_back(SCALARS, turned_scalars, 3)
+        log_subtract_store(EARLY, HALVES[1], sum_early, log_early, y_psum[EARLY][1][:])
+        for cols in HALVES:
+            subtract_and_store(SCALARS, cols, log_scalars[:, cols], y_sb[SCALARS][:, cols])
+        for cols in HALVES:
+            log_subtract_store(LATE, cols, sum_late, log_late, y_psum[LATE][0][:, cols])

@@ -56,8 +56,7 @@ def tile_picked_nce8_none_p_kernel(tc, x_words, x_scales, w1, offs, n1, n2, n3, 
         nc.sync.dma_start(w_raw[:, W_LOADS[0], :], w_rows[:, W_LOADS[0], :])
         offs_sb = keep.tile([P, S // PER_LIST_COLUMN], U16, name="offs_sb")
         nc.sync.dma_start(offs_sb[:], offs)
-        for q in range(4):
-            nc.sync.dma_start(key_scales[32 * q : 32 * q + 4, :].bitcast(I32), x_scales[0, 4 * q : 4 * q + 4, :].bitcast(I32))
+        nc.sync.dma_start(key_scales[0:P:8, :].bitcast(I32), x_scales[0].bitcast(I32))
         nc.sync.dma_start(w_raw[:, W_LOADS[1], :], w_rows[:, W_LOADS[1], :])
         key_words = sbuf("key_words", U32, T)
         nc.sync.dma_start(key_words[:].bitcast(I32), x_words[0].rearrange("p c r -> p (c r)").bitcast(I32))
@@ -70,8 +69,12 @@ def tile_picked_nce8_none_p_kernel(tc, x_words, x_scales, w1, offs, n1, n2, n3, 
         identity = sbuf("identity", F32, P)
         make_identity(nc, identity[:])
 
+        spread_scales = sbuf("spread_scales", U8)
+        nc.vector.tensor_copy(spread_scales[:], key_scales[:].indirect(offs_sb[:]))
         picked_scales = sbuf("picked_scales", U8)
-        nc.vector.tensor_copy(picked_scales[:], key_scales[:].indirect(offs_sb[:]))
+        nc.vector.memset(picked_scales[:].bitcast(I32), 0)
+        for q in range(4):
+            nc.scalar.dma_start(picked_scales[32 * q : 32 * q + 4, :].bitcast(I32), spread_scales[32 * q : 32 * q + 32 : 8, :].bitcast(I32))
 
         w_grouped = sbuf("w_grouped", BF16, PACK * N)
         grouped_view = w_grouped[:].rearrange("p (t m r) -> p m r t", t=TILES, r=PACK)
@@ -125,6 +128,7 @@ def tile_picked_nce8_none_p_kernel(tc, x_words, x_scales, w1, offs, n1, n2, n3, 
         shared_piece(1, LAST_QUARTERS[0])
         shared_piece(2, LAST_QUARTERS[1])
         nc.scalar.activation(e0[EARLY][:, HALVES[1]], y_psum[EARLY][1][:], EXP)
+        nc.sync.dma_start(e0_copy[EARLY][:, HALVES[1]], e0[EARLY][:, HALVES[1]])
 
         def scalar_lookup(t, i, spans):
             found = sbuf("found_%d_%d" % (t, i))
@@ -152,7 +156,6 @@ def tile_picked_nce8_none_p_kernel(tc, x_words, x_scales, w1, offs, n1, n2, n3, 
             return turned
 
         shared_n3 = vector_lookup(SHARED, 2)
-        nc.vector.tensor_copy(e0_copy[EARLY][:, HALVES[1]], e0[EARLY][:, HALVES[1]])
         shared_n2 = vector_lookup(SHARED, 1)
         nc.scalar.activation(e0[LATE][:, WHOLE], y_psum[LATE][0][:], EXP)
         nc.sync.dma_start(e0_copy[LATE][:], e0[LATE][:, WHOLE])
@@ -160,7 +163,7 @@ def tile_picked_nce8_none_p_kernel(tc, x_words, x_scales, w1, offs, n1, n2, n3, 
         turned_shared = turned_sum([e0[SHARED], shared_n1, shared_n2, shared_n3], 7, "turned_shared")
         nc.scalar.copy(y_sb[SCALARS][:, WHOLE], y_psum[SCALARS][0][:])
 
-        sum_early = lookup_and_add(EARLY, 0, e0_copy[EARLY], [WHOLE])
+        sum_early = lookup_and_add(EARLY, 0, e0_copy[EARLY], HALVES)
         sum_late = lookup_and_add(LATE, 0, e0_copy[LATE], [WHOLE])
         sum_early = lookup_and_add(EARLY, 1, sum_early, [WHOLE], tag="e0_copy_%d" % LATE)
         sum_late = lookup_and_add(LATE, 1, sum_late, [WHOLE])
@@ -176,13 +179,13 @@ def tile_picked_nce8_none_p_kernel(tc, x_words, x_scales, w1, offs, n1, n2, n3, 
         out_rows = out.rearrange("(p t) j -> p t j", t=TILES)
         loss = [sbuf("loss_%d" % t) for t in range(TILES)]
 
-        def log_turned_back(t, turned, number):
-            log_turned = sbuf("log_turned_%d" % t)
-            nc.scalar.activation(log_turned[:], turned[:], LN)
-            logs = bank(number, "log_bank_%d" % t, S)
-            for b in range(S // P):
-                cols = slice(P * b, P * (b + 1))
-                nc.tensor.transpose(logs[:, cols], log_turned[:, cols], identity[:])
+        log_turned = {t: sbuf("log_turned_%d" % t) for t in (SHARED, SCALARS)}
+
+        def log_turned_back(t, cols, turned, number):
+            nc.scalar.activation(log_turned[t][:, cols], turned[:, cols], LN)
+            logs = bank(number, "log_bank_%d" % number, S // 2)
+            for b in range(2):
+                nc.tensor.transpose(logs[:, P * b : P * (b + 1)], log_turned[t][:, cols.start + P * b : cols.start + P * (b + 1)], identity[:])
             return logs
 
         def subtract_and_store(t, cols, logs, scores):
@@ -195,12 +198,13 @@ def tile_picked_nce8_none_p_kernel(tc, x_words, x_scales, w1, offs, n1, n2, n3, 
 
         log_early = sbuf("log_early", tag="found_%d_%d" % (SHARED, 0))
         log_late = sbuf("log_late", tag="found_%d_%d" % (SCALARS, 2))
-        log_shared = log_turned_back(SHARED, turned_shared, 2)
+        shared_first = log_turned_back(SHARED, HALVES[0], turned_shared, 2)
         log_subtract_store(EARLY, HALVES[0], sum_early, log_early, y_psum[EARLY][0][:])
-        subtract_and_store(SHARED, WHOLE, log_shared[:], y_sb[SHARED][:, WHOLE])
-        log_scalars = log_turned_back(SCALARS, turned_scalars, 3)
+        subtract_and_store(SHARED, HALVES[0], shared_first[:], y_sb[SHARED][:, HALVES[0]])
+        shared_second = log_turned_back(SHARED, HALVES[1], turned_shared, 3)
         log_subtract_store(EARLY, HALVES[1], sum_early, log_early, y_psum[EARLY][1][:])
-        for cols in HALVES:
-            subtract_and_store(SCALARS, cols, log_scalars[:, cols], y_sb[SCALARS][:, cols])
-        for cols in HALVES:
+        subtract_and_store(SHARED, HALVES[1], shared_second[:], y_sb[SHARED][:, HALVES[1]])
+        scalars_logs = [log_turned_back(SCALARS, cols, turned_scalars, 6 + h) for h, cols in enumerate(HALVES)]
+        for h, cols in enumerate(HALVES):
             log_subtract_store(LATE, cols, sum_late, log_late, y_psum[LATE][0][:, cols])
+            subtract_and_store(SCALARS, cols, scalars_logs[h][:], y_sb[SCALARS][:, cols])

@@ -29,8 +29,8 @@ WHOLE = slice(0, S)
 HALVES = [slice(0, S // 2), slice(S // 2, S)]
 LAST_QUARTERS = [slice(S // 2, S // 2 + P), slice(S // 2 + P, S)]
 WINDOW = 2 * S
-VECTOR_ROWS = 96
-W_LOADS = [slice(0, PACK // 2), slice(PACK // 2, PACK)]
+VECTOR_ROWS = 92
+W_LOADS = [slice(0, 1), slice(1, PACK)]
 
 
 def tile_picked_nce8_none_p_kernel(tc, x_words, x_scales, w1, offs, n1, n2, n3, out):
@@ -74,7 +74,7 @@ def tile_picked_nce8_none_p_kernel(tc, x_words, x_scales, w1, offs, n1, n2, n3, 
         picked_scales = sbuf("picked_scales", U8)
         nc.vector.memset(picked_scales[:].bitcast(I32), 0)
         for q in range(4):
-            nc.scalar.dma_start(picked_scales[32 * q : 32 * q + 4, :].bitcast(I32), spread_scales[32 * q : 32 * q + 32 : 8, :].bitcast(I32))
+            nc.sync.dma_start(picked_scales[32 * q : 32 * q + 4, :].bitcast(I32), spread_scales[32 * q : 32 * q + 32 : 8, :].bitcast(I32))
 
         w_grouped = sbuf("w_grouped", BF16, PACK * N)
         grouped_view = w_grouped[:].rearrange("p (t m r) -> p m r t", t=TILES, r=PACK)
@@ -126,9 +126,10 @@ def tile_picked_nce8_none_p_kernel(tc, x_words, x_scales, w1, offs, n1, n2, n3, 
         nc.scalar.activation(e0[EARLY][:, HALVES[0]], y_psum[EARLY][0][:], EXP)
         nc.vector.tensor_copy(e0_copy[EARLY][:, HALVES[0]], e0[EARLY][:, HALVES[0]])
         shared_piece(1, LAST_QUARTERS[0])
-        shared_piece(2, LAST_QUARTERS[1])
+        nc.scalar.activation(e0[SHARED][:, LAST_QUARTERS[1]], y_psum[SHARED][2][:], EXP)
         nc.scalar.activation(e0[EARLY][:, HALVES[1]], y_psum[EARLY][1][:], EXP)
         nc.sync.dma_start(e0_copy[EARLY][:, HALVES[1]], e0[EARLY][:, HALVES[1]])
+        nc.scalar.copy(y_sb[SHARED][:, LAST_QUARTERS[1]], y_psum[SHARED][2][:])
 
         def scalar_lookup(t, i, spans):
             found = sbuf("found_%d_%d" % (t, i))
@@ -204,7 +205,7 @@ def tile_picked_nce8_none_p_kernel(tc, x_words, x_scales, w1, offs, n1, n2, n3, 
         shared_second = log_turned_back(SHARED, HALVES[1], turned_shared, 3)
         log_subtract_store(EARLY, HALVES[1], sum_early, log_early, y_psum[EARLY][1][:])
         subtract_and_store(SHARED, HALVES[1], shared_second[:], y_sb[SHARED][:, HALVES[1]])
-        scalars_logs = [log_turned_back(SCALARS, cols, turned_scalars, 6 + h) for h, cols in enumerate(HALVES)]
         for h, cols in enumerate(HALVES):
+            scalars_logs = log_turned_back(SCALARS, cols, turned_scalars, 6 + h)
             log_subtract_store(LATE, cols, sum_late, log_late, y_psum[LATE][0][:, cols])
-            subtract_and_store(SCALARS, cols, scalars_logs[h][:], y_sb[SCALARS][:, cols])
+            subtract_and_store(SCALARS, cols, scalars_logs[:], y_sb[SCALARS][:, cols])

@@ -79,16 +79,23 @@ def tile_picked_nce8_none_p_kernel(tc, x_words, x_scales, w1, offs, n1, n2, n3, 
         w_grouped = sbuf("w_grouped", BF16, PACK * N)
         grouped_view = w_grouped[:].rearrange("p (t m r) -> p m r t", t=TILES, r=PACK)
         raw_view = w_raw[:].rearrange("p r (m t) -> p m r t", t=TILES)
-        nc.vector.tensor_copy(grouped_view[:, :VECTOR_ROWS], raw_view[:, :VECTOR_ROWS])
+        nc.vector.tensor_copy(grouped_view[:, :, :, :2], raw_view[:, :, :, :2])
         for planes in W_LOADS:
-            nc.scalar.activation(grouped_view[:, VECTOR_ROWS:, planes], raw_view[:, VECTOR_ROWS:, planes], COPY)
-        w_codes = sbuf("w_codes", U32, N)
+            nc.scalar.activation(grouped_view[:, :, planes, 2:], raw_view[:, :, planes, 2:], COPY)
         w_scales = sbuf("w_scales", U8, N)
-        nc.vector.quantize_mx(out=w_codes[:].bitcast(FP8X4), scales=w_scales[:], in_=w_grouped[:])
+
+        def quantise_pair(pair, tag):
+            codes = sbuf("w_codes_%d" % pair, U32, N // 2, tag=tag)
+            cols = slice(pair * N // 2, (pair + 1) * N // 2)
+            nc.vector.quantize_mx(out=codes[:].bitcast(FP8X4), scales=w_scales[:, cols], in_=w_grouped[:, PACK * cols.start : PACK * cols.stop])
+            return codes
+
+        w_codes = [quantise_pair(0, None)]
 
         picked_words = sbuf("picked_words", U32)
         for cols in HALVES:
             nc.vector.tensor_copy(picked_words[:, cols], key_words[:].indirect(entries(offs_sb, cols)))
+        w_codes.append(quantise_pair(1, "key_words"))
 
         pieces = [
             (SHARED, HALVES[0]),
@@ -105,7 +112,7 @@ def tile_picked_nce8_none_p_kernel(tc, x_words, x_scales, w1, offs, n1, n2, n3, 
             scores = bank(number, "y_piece_%d" % number, cols.stop - cols.start)
             nc.tensor.matmul_mx(
                 out=scores[:],
-                lhsT=w_codes[:, rows].bitcast(FP8X4),
+                lhsT=w_codes[t // 2][:, P * (t % 2) : P * (t % 2 + 1)].bitcast(FP8X4),
                 lhsT_scale=w_scales[:, rows],
                 rhs=picked_words[:, cols].bitcast(FP8X4),
                 rhs_scale=picked_scales[:, cols],

@@ -30,7 +30,7 @@ HALVES = [slice(0, S // 2), slice(S // 2, S)]
 LAST_QUARTERS = [slice(S // 2, S // 2 + P), slice(S // 2 + P, S)]
 WINDOW = 2 * S
 VECTOR_ROWS = 92
-W_LOADS = [slice(0, 1), slice(1, PACK)]
+W_LOADS = [slice(0, 2), slice(2, PACK)]
 
 
 def tile_picked_nce8_none_p_kernel(tc, x_words, x_scales, w1, offs, n1, n2, n3, out):

@@ -74,7 +74,7 @@ def tile_picked_nce8_none_p_kernel(tc, x_words, x_scales, w1, offs, n1, n2, n3, 
         picked_scales = sbuf("picked_scales", U8)
         nc.vector.memset(picked_scales[:].bitcast(I32), 0)
         for q in range(4):
-            nc.sync.dma_start(picked_scales[32 * q : 32 * q + 4, :].bitcast(I32), spread_scales[32 * q : 32 * q + 32 : 8, :].bitcast(I32))
+            nc.scalar.dma_start(picked_scales[32 * q : 32 * q + 4, :].bitcast(I32), spread_scales[32 * q : 32 * q + 32 : 8, :].bitcast(I32))
 
         w_grouped = sbuf("w_grouped", BF16, PACK * N)
         grouped_view = w_grouped[:].rearrange("p (t m r) -> p m r t", t=TILES, r=PACK)
@@ -176,7 +176,7 @@ def tile_picked_nce8_none_p_kernel(tc, x_words, x_scales, w1, offs, n1, n2, n3, 
         sum_early = lookup_and_add(EARLY, 1, sum_early, [WHOLE], tag="e0_copy_%d" % LATE)
         sum_late = lookup_and_add(LATE, 1, sum_late, [WHOLE])
         sum_early = lookup_and_add(EARLY, 2, sum_early, [WHOLE])
-        sum_late = lookup_and_add(LATE, 2, sum_late, HALVES)
+        sum_late = lookup_and_add(LATE, 2, sum_late, [WHOLE])
 
         scalars_n1 = scalar_lookup(SCALARS, 0, [WHOLE])
         scalars_n2 = scalar_lookup(SCALARS, 1, [WHOLE])

@@ -170,6 +170,7 @@ def tile_picked_nce8_none_p_kernel(tc, x_words, x_scales, w1, offs, n1, n2, n3, 
         shared_n1 = scalar_lookup(SHARED, 0, [WHOLE])
         turned_shared = turned_sum([e0[SHARED], shared_n1, shared_n2, shared_n3], 7, "turned_shared")
         nc.scalar.copy(y_sb[SCALARS][:, WHOLE], y_psum[SCALARS][0][:])
+        nc.scalar.activation(e0[SCALARS][:], y_psum[SCALARS][0][:], EXP)
 
         sum_early = lookup_and_add(EARLY, 0, e0_copy[EARLY], HALVES)
         sum_late = lookup_and_add(LATE, 0, e0_copy[LATE], [WHOLE])
@@ -180,20 +181,18 @@ def tile_picked_nce8_none_p_kernel(tc, x_words, x_scales, w1, offs, n1, n2, n3, 
 
         scalars_n1 = scalar_lookup(SCALARS, 0, [WHOLE])
         scalars_n2 = scalar_lookup(SCALARS, 1, [WHOLE])
-        nc.scalar.activation(e0[SCALARS][:], y_sb[SCALARS][:, WHOLE], EXP)
         scalars_n3 = scalar_lookup(SCALARS, 2, HALVES)
         turned_scalars = turned_sum([e0[SCALARS], scalars_n1, scalars_n2, scalars_n3], 0, "turned_scalars")
 
         out_rows = out.rearrange("(p t) j -> p t j", t=TILES)
         loss = [sbuf("loss_%d" % t) for t in range(TILES)]
 
-        log_turned = {t: sbuf("log_turned_%d" % t) for t in (SHARED, SCALARS)}
-
-        def log_turned_back(t, cols, turned, number):
-            nc.scalar.activation(log_turned[t][:, cols], turned[:, cols], LN)
+        def log_turned_back(t, cols, turned, number, tag=None):
+            log_turned = sbuf("log_turned_%d" % number, F32, S // 2, tag=tag)
+            nc.scalar.activation(log_turned[:], turned[:, cols], LN)
             logs = bank(number, "log_bank_%d" % number, S // 2)
             for b in range(2):
-                nc.tensor.transpose(logs[:, P * b : P * (b + 1)], log_turned[t][:, cols.start + P * b : cols.start + P * (b + 1)], identity[:])
+                nc.tensor.transpose(logs[:, P * b : P * (b + 1)], log_turned[:, P * b : P * (b + 1)], identity[:])
             return logs
 
         def subtract_and_store(t, cols, logs, scores):
@@ -209,10 +208,10 @@ def tile_picked_nce8_none_p_kernel(tc, x_words, x_scales, w1, offs, n1, n2, n3, 
         shared_first = log_turned_back(SHARED, HALVES[0], turned_shared, 2)
         log_subtract_store(EARLY, HALVES[0], sum_early, log_early, y_psum[EARLY][0][:])
         subtract_and_store(SHARED, HALVES[0], shared_first[:], y_sb[SHARED][:, HALVES[0]])
-        shared_second = log_turned_back(SHARED, HALVES[1], turned_shared, 3)
+        shared_second = log_turned_back(SHARED, HALVES[1], turned_shared, 3, tag="e0_copy_%d" % LATE)
         log_subtract_store(EARLY, HALVES[1], sum_early, log_early, y_psum[EARLY][1][:])
         subtract_and_store(SHARED, HALVES[1], shared_second[:], y_sb[SHARED][:, HALVES[1]])
         for h, cols in enumerate(HALVES):
-            scalars_logs = log_turned_back(SCALARS, cols, turned_scalars, 6 + h)
+            scalars_logs = log_turned_back(SCALARS, cols, turned_scalars, 6 + h, tag=("e0_%d" % EARLY, "sum_%d_1" % LATE)[h])
             log_subtract_store(LATE, cols, sum_late, log_late, y_psum[LATE][0][:, cols])
             subtract_and_store(SCALARS, cols, scalars_logs[:], y_sb[SCALARS][:, cols])

@@ -97,29 +97,27 @@ def tile_picked_nce8_none_p_kernel(tc, x_words, x_scales, w1, offs, n1, n2, n3, 
             nc.vector.tensor_copy(picked_words[:, cols], key_words[:].indirect(entries(offs_sb, cols)))
         w_codes.append(quantise_pair(1, "key_words"))
 
-        pieces = [
-            (SHARED, HALVES[0]),
-            (EARLY, HALVES[0]),
-            (SHARED, LAST_QUARTERS[0]),
-            (SHARED, LAST_QUARTERS[1]),
-            (EARLY, HALVES[1]),
-            (LATE, WHOLE),
-            (SCALARS, WHOLE),
-        ]
         y_psum = {t: [] for t in range(TILES)}
-        for number, (t, cols) in enumerate(pieces):
-            rows = slice(P * t, P * (t + 1))
-            scores = bank(number, "y_piece_%d" % number, cols.stop - cols.start)
+
+        def product(t, cols, number):
+            scores = bank(number, "y_%d_from_%d" % (t, cols.start), cols.stop - cols.start)
             nc.tensor.matmul_mx(
                 out=scores[:],
                 lhsT=w_codes[t // 2][:, P * (t % 2) : P * (t % 2 + 1)].bitcast(FP8X4),
-                lhsT_scale=w_scales[:, rows],
+                lhsT_scale=w_scales[:, P * t : P * (t + 1)],
                 rhs=picked_words[:, cols].bitcast(FP8X4),
                 rhs_scale=picked_scales[:, cols],
                 start=True,
                 stop=True,
             )
             y_psum[t].append(scores)
+
+        product(SHARED, HALVES[0], 0)
+        product(EARLY, HALVES[0], 1)
+        product(SHARED, LAST_QUARTERS[0], 2)
+        product(SHARED, LAST_QUARTERS[1], 3)
+        product(EARLY, HALVES[1], 4)
+        product(LATE, WHOLE, 5)
 
         e0 = [sbuf("e0_%d" % t, F32, S if t == SCALARS else WINDOW) for t in range(TILES)]
         y_sb = {t: sbuf("y_%d" % t, F32, WINDOW) for t in (SHARED, SCALARS)}
@@ -137,6 +135,8 @@ def tile_picked_nce8_none_p_kernel(tc, x_words, x_scales, w1, offs, n1, n2, n3, 
         nc.scalar.activation(e0[EARLY][:, HALVES[1]], y_psum[EARLY][1][:], EXP)
         nc.sync.dma_start(e0_copy[EARLY][:, HALVES[1]], e0[EARLY][:, HALVES[1]])
         nc.scalar.copy(y_sb[SHARED][:, LAST_QUARTERS[1]], y_psum[SHARED][2][:])
+        product(SCALARS, HALVES[0], 3)
+        product(SCALARS, HALVES[1], 6)
 
         def scalar_lookup(t, i, spans):
             found = sbuf("found_%d_%d" % (t, i))
@@ -144,8 +144,8 @@ def tile_picked_nce8_none_p_kernel(tc, x_words, x_scales, w1, offs, n1, n2, n3, 
                 nc.scalar.activation(found[:, cols], y_sb[t][:].indirect(entries(negatives[i], cols)), EXP)
             return found
 
-        def vector_lookup(t, i):
-            found = sbuf("found_%d_%d" % (t, i))
+        def vector_lookup(t, i, tag=None):
+            found = sbuf("found_%d_%d" % (t, i), tag=tag)
             nc.vector.tensor_copy(found[:], e0[t][:].indirect(negatives[i][:]))
             return found
 
@@ -164,13 +164,15 @@ def tile_picked_nce8_none_p_kernel(tc, x_words, x_scales, w1, offs, n1, n2, n3, 
             return turned
 
         shared_n3 = vector_lookup(SHARED, 2)
-        shared_n2 = vector_lookup(SHARED, 1)
+        nc.vector.tensor_copy(y_sb[SCALARS][:, HALVES[0]], y_psum[SCALARS][0][:])
+        shared_n2 = vector_lookup(SHARED, 1, tag="picked_words")
         nc.scalar.activation(e0[LATE][:, WHOLE], y_psum[LATE][0][:], EXP)
         nc.sync.dma_start(e0_copy[LATE][:], e0[LATE][:, WHOLE])
         shared_n1 = scalar_lookup(SHARED, 0, [WHOLE])
         turned_shared = turned_sum([e0[SHARED], shared_n1, shared_n2, shared_n3], 7, "turned_shared")
-        nc.scalar.copy(y_sb[SCALARS][:, WHOLE], y_psum[SCALARS][0][:])
-        nc.scalar.activation(e0[SCALARS][:], y_psum[SCALARS][0][:], EXP)
+        nc.scalar.copy(y_sb[SCALARS][:, HALVES[1]], y_psum[SCALARS][1][:])
+        for h in (1, 0):
+            nc.scalar.activation(e0[SCALARS][:, HALVES[h]], y_psum[SCALARS][h][:], EXP)
 
         sum_early = lookup_and_add(EARLY, 0, e0_copy[EARLY], HALVES)
         sum_late = lookup_and_add(LATE, 0, e0_copy[LATE], [WHOLE])

@@ -121,7 +121,8 @@ def tile_picked_nce8_none_p_kernel(tc, x_words, x_scales, w1, offs, n1, n2, n3, 
 
         e0 = [sbuf("e0_%d" % t, F32, S if t == SCALARS else WINDOW) for t in range(TILES)]
         y_sb = {t: sbuf("y_%d" % t, F32, WINDOW) for t in (SHARED, SCALARS)}
-        e0_copy = {t: sbuf("e0_copy_%d" % t) for t in (EARLY, LATE)}
+        e0_copy = {EARLY: sbuf("e0_copy_%d" % EARLY)}
+        late_seeds = [sbuf("late_seed_%d" % h, F32, S // 2) for h in range(2)]
 
         def shared_piece(piece, cols):
             nc.scalar.activation(e0[SHARED][:, cols], y_psum[SHARED][piece][:], EXP)
@@ -166,8 +167,10 @@ def tile_picked_nce8_none_p_kernel(tc, x_words, x_scales, w1, offs, n1, n2, n3, 
         shared_n3 = vector_lookup(SHARED, 2)
         nc.vector.tensor_copy(y_sb[SCALARS][:, HALVES[0]], y_psum[SCALARS][0][:])
         shared_n2 = vector_lookup(SHARED, 1, tag="picked_words")
-        nc.scalar.activation(e0[LATE][:, WHOLE], y_psum[LATE][0][:], EXP)
-        nc.sync.dma_start(e0_copy[LATE][:], e0[LATE][:, WHOLE])
+        nc.scalar.activation(e0[LATE][:, HALVES[0]], y_psum[LATE][0][:, HALVES[0]], EXP)
+        nc.sync.dma_start(late_seeds[0][:], e0[LATE][:, HALVES[0]])
+        nc.scalar.activation(late_seeds[1][:], y_psum[LATE][0][:, HALVES[1]], EXP)
+        nc.sync.dma_start(e0[LATE][:, HALVES[1]], late_seeds[1][:])
         shared_n1 = scalar_lookup(SHARED, 0, [WHOLE])
         turned_shared = turned_sum([e0[SHARED], shared_n1, shared_n2, shared_n3], 7, "turned_shared")
         nc.scalar.copy(y_sb[SCALARS][:, HALVES[1]], y_psum[SCALARS][1][:])
@@ -175,8 +178,10 @@ def tile_picked_nce8_none_p_kernel(tc, x_words, x_scales, w1, offs, n1, n2, n3, 
             nc.scalar.activation(e0[SCALARS][:, HALVES[h]], y_psum[SCALARS][h][:], EXP)
 
         sum_early = lookup_and_add(EARLY, 0, e0_copy[EARLY], HALVES)
-        sum_late = lookup_and_add(LATE, 0, e0_copy[LATE], [WHOLE])
-        sum_early = lookup_and_add(EARLY, 1, sum_early, [WHOLE], tag="e0_copy_%d" % LATE)
+        sum_late = sbuf("sum_%d_0" % LATE)
+        for h, cols in enumerate(HALVES):
+            nc.vector.tensor_tensor(sum_late[:, cols], e0[LATE][:].indirect(entries(negatives[0], cols)), late_seeds[h][:], ADD)
+        sum_early = lookup_and_add(EARLY, 1, sum_early, [WHOLE], tag="late_seed_0")
         sum_late = lookup_and_add(LATE, 1, sum_late, [WHOLE])
         sum_early = lookup_and_add(EARLY, 2, sum_early, [WHOLE])
         sum_late = lookup_and_add(LATE, 2, sum_late, [WHOLE])
@@ -210,7 +215,7 @@ def tile_picked_nce8_none_p_kernel(tc, x_words, x_scales, w1, offs, n1, n2, n3, 
         shared_first = log_turned_back(SHARED, HALVES[0], turned_shared, 2)
         log_subtract_store(EARLY, HALVES[0], sum_early, log_early, y_psum[EARLY][0][:])
         subtract_and_store(SHARED, HALVES[0], shared_first[:], y_sb[SHARED][:, HALVES[0]])
-        shared_second = log_turned_back(SHARED, HALVES[1], turned_shared, 3, tag="e0_copy_%d" % LATE)
+        shared_second = log_turned_back(SHARED, HALVES[1], turned_shared, 3, tag="late_seed_0")
         log_subtract_store(EARLY, HALVES[1], sum_early, log_early, y_psum[EARLY][1][:])
         subtract_and_store(SHARED, HALVES[1], shared_second[:], y_sb[SHARED][:, HALVES[1]])
         for h, cols in enumerate(HALVES):

@@ -119,8 +119,8 @@ def tile_picked_nce8_none_p_kernel(tc, x_words, x_scales, w1, offs, n1, n2, n3, 
         product(EARLY, HALVES[1], 4)
         product(LATE, WHOLE, 5)
 
-        e0 = [sbuf("e0_%d" % t, F32, S if t == SCALARS else WINDOW) for t in range(TILES)]
-        y_sb = {t: sbuf("y_%d" % t, F32, WINDOW) for t in (SHARED, SCALARS)}
+        e0 = [sbuf("e0_%d" % t, F32, WINDOW) for t in range(TILES)]
+        y_sb = {t: sbuf("y_%d" % t) for t in (SHARED, SCALARS)}
         e0_copy = {EARLY: sbuf("e0_copy_%d" % EARLY)}
         late_seeds = [sbuf("late_seed_%d" % h, F32, S // 2) for h in range(2)]
 
@@ -139,10 +139,9 @@ def tile_picked_nce8_none_p_kernel(tc, x_words, x_scales, w1, offs, n1, n2, n3, 
         product(SCALARS, HALVES[0], 3)
         product(SCALARS, HALVES[1], 6)
 
-        def scalar_lookup(t, i, spans):
-            found = sbuf("found_%d_%d" % (t, i))
+        def scalar_lookup(t, i, spans, found):
             for cols in spans:
-                nc.scalar.activation(found[:, cols], y_sb[t][:].indirect(entries(negatives[i], cols)), EXP)
+                nc.scalar.activation(found[:, cols], e0[t][:].indirect(entries(negatives[i], cols)), COPY)
             return found
 
         def vector_lookup(t, i, tag=None):
@@ -150,75 +149,99 @@ def tile_picked_nce8_none_p_kernel(tc, x_words, x_scales, w1, offs, n1, n2, n3, 
             nc.vector.tensor_copy(found[:], e0[t][:].indirect(negatives[i][:]))
             return found
 
-        def lookup_and_add(t, i, total, spans, tag=None):
-            grown = sbuf("sum_%d_%d" % (t, i), tag=tag)
+        def lookup_and_add(t, i, total, spans, grown):
             for cols in spans:
                 nc.vector.tensor_tensor(grown[:, cols], e0[t][:].indirect(entries(negatives[i], cols)), total[:, cols], ADD)
             return grown
 
-        def turned_sum(terms, number, name):
-            turned = bank(number, name, S)
-            for b in range(S // P):
-                cols = slice(P * b, P * (b + 1))
-                for n, term in enumerate(terms):
-                    nc.tensor.matmul(turned[:, cols], term[:, cols], identity[:], is_transpose=True, start=(n == 0), stop=(n == len(terms) - 1))
+        def turned_sum(terms, number, name, width):
+            turned = bank(number, name, width)
+            blocks = width // P
+            for n, term in enumerate(terms):
+                for b in range(blocks):
+                    cols = slice(P * b, P * (b + 1))
+                    nc.tensor.matmul(turned[:, cols], term[:, cols], identity[:], is_transpose=True, start=(n == 0 and b == 0), stop=(n == len(terms) - 1 and b == blocks - 1))
             return turned
+
+        out_rows = out.rearrange("(p t) j -> p t j", t=TILES)
+        loss = {t: sbuf("loss_%d" % t) for t in (EARLY, LATE, SCALARS)}
+
+        def subtract(t, cols, logs, scores):
+            nc.vector.tensor_tensor(loss[t][:, cols], logs, scores, SUB)
+
+        def store(t, cols):
+            nc.sync.dma_start(out_rows[:, t, cols], loss[t][:, cols])
 
         shared_n3 = vector_lookup(SHARED, 2)
         nc.vector.tensor_copy(y_sb[SCALARS][:, HALVES[0]], y_psum[SCALARS][0][:])
-        shared_n2 = vector_lookup(SHARED, 1, tag="picked_words")
+        shared_n2 = sbuf("shared_n2", tag="picked_words")
+        nc.vector.tensor_copy(shared_n2[:, HALVES[0]], e0[SHARED][:].indirect(entries(negatives[1], HALVES[0])))
         nc.scalar.activation(e0[LATE][:, HALVES[0]], y_psum[LATE][0][:, HALVES[0]], EXP)
         nc.sync.dma_start(late_seeds[0][:], e0[LATE][:, HALVES[0]])
         nc.scalar.activation(late_seeds[1][:], y_psum[LATE][0][:, HALVES[1]], EXP)
         nc.sync.dma_start(e0[LATE][:, HALVES[1]], late_seeds[1][:])
-        shared_n1 = scalar_lookup(SHARED, 0, [WHOLE])
-        turned_shared = turned_sum([e0[SHARED], shared_n1, shared_n2, shared_n3], 7, "turned_shared")
-        nc.scalar.copy(y_sb[SCALARS][:, HALVES[1]], y_psum[SCALARS][1][:])
+        shared_n1 = scalar_lookup(SHARED, 0, [WHOLE], sbuf("shared_n1"))
+        scalar_lookup(SHARED, 1, HALVES[1:], shared_n2)
+        turned_shared = turned_sum([e0[SHARED], shared_n3, shared_n1, shared_n2], 7, "turned_shared", S)
         for h in (1, 0):
             nc.scalar.activation(e0[SCALARS][:, HALVES[h]], y_psum[SCALARS][h][:], EXP)
 
-        sum_early = lookup_and_add(EARLY, 0, e0_copy[EARLY], HALVES)
-        sum_late = sbuf("sum_%d_0" % LATE)
+        sum_early = lookup_and_add(EARLY, 0, e0_copy[EARLY], HALVES, sbuf("sum_early_0"))
+        sum_late = sbuf("sum_late_0")
         for h, cols in enumerate(HALVES):
             nc.vector.tensor_tensor(sum_late[:, cols], e0[LATE][:].indirect(entries(negatives[0], cols)), late_seeds[h][:], ADD)
-        sum_early = lookup_and_add(EARLY, 1, sum_early, [WHOLE], tag="late_seed_0")
-        sum_late = lookup_and_add(LATE, 1, sum_late, [WHOLE])
-        sum_early = lookup_and_add(EARLY, 2, sum_early, [WHOLE])
-        sum_late = lookup_and_add(LATE, 2, sum_late, [WHOLE])
+        sum_early = lookup_and_add(EARLY, 1, sum_early, [WHOLE], sbuf("sum_early_1", tag="late_seed_0"))
 
-        scalars_n1 = scalar_lookup(SCALARS, 0, [WHOLE])
-        scalars_n2 = scalar_lookup(SCALARS, 1, [WHOLE])
-        scalars_n3 = scalar_lookup(SCALARS, 2, HALVES)
-        turned_scalars = turned_sum([e0[SCALARS], scalars_n1, scalars_n2, scalars_n3], 0, "turned_scalars")
-
-        out_rows = out.rearrange("(p t) j -> p t j", t=TILES)
-        loss = [sbuf("loss_%d" % t) for t in range(TILES)]
-
-        def log_turned_back(t, cols, turned, number, tag=None):
-            log_turned = sbuf("log_turned_%d" % number, F32, S // 2, tag=tag)
-            nc.scalar.activation(log_turned[:], turned[:, cols], LN)
-            logs = bank(number, "log_bank_%d" % number, S // 2)
+        def log_half_back(log_turned, turned, number, name):
+            nc.scalar.activation(log_turned, turned, LN)
+            logs = bank(number, "logs_" + name, S // 2)
             for b in range(2):
                 nc.tensor.transpose(logs[:, P * b : P * (b + 1)], log_turned[:, P * b : P * (b + 1)], identity[:])
             return logs
 
-        def subtract_and_store(t, cols, logs, scores):
-            nc.vector.tensor_tensor(loss[t][:, cols], logs, scores, SUB)
-            nc.sync.dma_start(out_rows[:, t, cols], loss[t][:, cols])
-
-        def log_subtract_store(t, cols, total, logs, scores):
-            nc.scalar.activation(logs[:, cols], total[:, cols], LN)
-            subtract_and_store(t, cols, logs[:, cols], scores)
-
-        log_early = sbuf("log_early", tag="found_%d_%d" % (SHARED, 0))
-        log_late = sbuf("log_late", tag="found_%d_%d" % (SCALARS, 2))
-        shared_first = log_turned_back(SHARED, HALVES[0], turned_shared, 2)
-        log_subtract_store(EARLY, HALVES[0], sum_early, log_early, y_psum[EARLY][0][:])
-        subtract_and_store(SHARED, HALVES[0], shared_first[:], y_sb[SHARED][:, HALVES[0]])
-        shared_second = log_turned_back(SHARED, HALVES[1], turned_shared, 3, tag="late_seed_0")
-        log_subtract_store(EARLY, HALVES[1], sum_early, log_early, y_psum[EARLY][1][:])
-        subtract_and_store(SHARED, HALVES[1], shared_second[:], y_sb[SHARED][:, HALVES[1]])
+        log_turned_shared = sbuf("log_turned_shared")
+        loss[SHARED] = sbuf("loss_shared", tag="late_seed_1")
         for h, cols in enumerate(HALVES):
-            scalars_logs = log_turned_back(SCALARS, cols, turned_scalars, 6 + h, tag=("e0_%d" % EARLY, "sum_%d_1" % LATE)[h])
-            log_subtract_store(LATE, cols, sum_late, log_late, y_psum[LATE][0][:, cols])
-            subtract_and_store(SCALARS, cols, scalars_logs[:], y_sb[SCALARS][:, cols])
+            logs = log_half_back(log_turned_shared[:, cols], turned_shared[:, cols], (0, 2)[h], "shared_%d" % h)
+            subtract(SHARED, cols, logs[:], y_sb[SHARED][:, cols])
+        store(SHARED, WHOLE)
+        sum_early = lookup_and_add(EARLY, 2, sum_early, [WHOLE], sbuf("sum_early_2", tag="log_turned_shared"))
+        sum_late = lookup_and_add(LATE, 1, sum_late, [WHOLE], sbuf("sum_late_1", tag="y_%d" % SHARED))
+
+        found = sbuf("found_scalars", F32, 2 * S + S // 2, tag="e0_copy_%d" % EARLY)
+        terms = [e0[SCALARS]] + [scalar_lookup(SCALARS, i, [WHOLE], found[:, S * i : S * (i + 1)]) for i in range(2)]
+        scalar_lookup(SCALARS, 2, HALVES[:1], found[:, 2 * S :])
+
+        log_early = sbuf("log_early")
+        nc.scalar.activation(log_early[:], sum_early[:], LN)
+        for h, cols in enumerate(HALVES):
+            subtract(EARLY, cols, log_early[:, cols], y_psum[EARLY][h][:])
+        store(EARLY, WHOLE)
+        sum_late = lookup_and_add(LATE, 2, sum_late, HALVES, sbuf("sum_late_2", tag="log_turned_shared"))
+
+        after_early = sbuf("after_early", tag="late_seed_0")
+        scalar_lookup(SCALARS, 2, HALVES[1:], after_early)
+        turned = [bank(3, "turned_first", S // 2), bank(7, "turned_second", S // 2)]
+        for n in range(4):
+            for h, cols in enumerate(HALVES):
+                term = terms[n] if n < 3 else (found[:, 2 * S :], after_early)[h]
+                for b in range(2):
+                    block = term[:, cols.start + P * b : cols.start + P * (b + 1)]
+                    nc.tensor.matmul(turned[h][:, P * b : P * (b + 1)], block, identity[:], is_transpose=True, start=(n == 0 and b == 0), stop=(n == 3 and b == 1))
+        log_turned_first = sbuf("log_turned_first", F32, S // 2, tag="e0_%d" % EARLY)
+        logs_first = log_half_back(log_turned_first[:], turned[0][:], 0, "first")
+        subtract(SCALARS, HALVES[0], logs_first[:], y_sb[SCALARS][:, HALVES[0]])
+        store(SCALARS, HALVES[0])
+        y_second = after_early[:, HALVES[0]]
+        nc.scalar.copy(y_second, y_psum[SCALARS][1][:])
+        log_turned_second = sbuf("log_turned_second", F32, S // 2)
+        logs_second = log_half_back(log_turned_second[:], turned[1][:], 2, "second")
+        log_late = sbuf("log_late", tag="e0_%d" % EARLY)
+        for cols in HALVES:
+            nc.scalar.activation(log_late[:, cols], sum_late[:, cols], LN)
+        subtract(LATE, HALVES[0], log_late[:, HALVES[0]], y_psum[LATE][0][:, HALVES[0]])
+        store(LATE, HALVES[0])
+        subtract(SCALARS, HALVES[1], logs_second[:], y_second)
+        store(SCALARS, HALVES[1])
+        subtract(LATE, HALVES[1], log_late[:, HALVES[1]], y_psum[LATE][0][:, HALVES[1]])
+        store(LATE, HALVES[1])

@@ -199,49 +199,50 @@ def tile_picked_nce8_none_p_kernel(tc, x_words, x_scales, w1, offs, n1, n2, n3, 
                 nc.tensor.transpose(logs[:, P * b : P * (b + 1)], log_turned[:, P * b : P * (b + 1)], identity[:])
             return logs
 
+        late_middle = sbuf("sum_late_1")
+        lookup_and_add(LATE, 1, sum_late, HALVES[:1], late_middle)
         log_turned_shared = sbuf("log_turned_shared")
-        loss[SHARED] = sbuf("loss_shared", tag="late_seed_1")
+        after_seed = sbuf("after_seed", F32, S + S // 2, tag="late_seed_1")
+        loss[SHARED], y_second = after_seed[:, :S], after_seed[:, S:]
+        nc.vector.tensor_copy(y_second[:, :P], y_psum[SCALARS][1][:, :P])
         for h, cols in enumerate(HALVES):
             logs = log_half_back(log_turned_shared[:, cols], turned_shared[:, cols], (0, 2)[h], "shared_%d" % h)
             subtract(SHARED, cols, logs[:], y_sb[SHARED][:, cols])
         store(SHARED, WHOLE)
-        sum_early = lookup_and_add(EARLY, 2, sum_early, [WHOLE], sbuf("sum_early_2", tag="log_turned_shared"))
-        sum_late = lookup_and_add(LATE, 1, sum_late, [WHOLE], sbuf("sum_late_1", tag="y_%d" % SHARED))
+        sum_early = lookup_and_add(EARLY, 2, sum_early, [WHOLE], sbuf("sum_early_2"))
+        lookup_and_add(LATE, 1, sum_late, HALVES[1:], late_middle)
+        sum_late = lookup_and_add(LATE, 2, late_middle, HALVES, sbuf("sum_late_2"))
 
-        found = sbuf("found_scalars", F32, 2 * S + S // 2, tag="e0_copy_%d" % EARLY)
-        terms = [e0[SCALARS]] + [scalar_lookup(SCALARS, i, [WHOLE], found[:, S * i : S * (i + 1)]) for i in range(2)]
-        scalar_lookup(SCALARS, 2, HALVES[:1], found[:, 2 * S :])
+        nc.scalar.copy(y_second[:, P:], y_psum[SCALARS][1][:, P:])
+        found = sbuf("found_scalars", F32, 3 * S, tag="e0_copy_%d" % EARLY)
+        terms = [e0[SCALARS]] + [scalar_lookup(SCALARS, i, [WHOLE] if i < 2 else HALVES, found[:, S * i : S * (i + 1)]) for i in range(3)]
+        turned = [bank(3, "turned_first", S // 2), bank(7, "turned_second", S // 2)]
+        for n, term in enumerate(terms):
+            for h, cols in enumerate(HALVES):
+                for b in range(2):
+                    block = term[:, cols.start + P * b : cols.start + P * (b + 1)]
+                    nc.tensor.matmul(turned[h][:, P * b : P * (b + 1)], block, identity[:], is_transpose=True, start=(n == 0 and b == 0), stop=(n == 3 and b == 1))
 
         log_early = sbuf("log_early")
         nc.scalar.activation(log_early[:], sum_early[:], LN)
         for h, cols in enumerate(HALVES):
             subtract(EARLY, cols, log_early[:, cols], y_psum[EARLY][h][:])
-        store(EARLY, WHOLE)
-        sum_late = lookup_and_add(LATE, 2, sum_late, HALVES, sbuf("sum_late_2", tag="log_turned_shared"))
-
-        after_early = sbuf("after_early", tag="late_seed_0")
-        scalar_lookup(SCALARS, 2, HALVES[1:], after_early)
-        turned = [bank(3, "turned_first", S // 2), bank(7, "turned_second", S // 2)]
-        for n in range(4):
-            for h, cols in enumerate(HALVES):
-                term = terms[n] if n < 3 else (found[:, 2 * S :], after_early)[h]
-                for b in range(2):
-                    block = term[:, cols.start + P * b : cols.start + P * (b + 1)]
-                    nc.tensor.matmul(turned[h][:, P * b : P * (b + 1)], block, identity[:], is_transpose=True, start=(n == 0 and b == 0), stop=(n == 3 and b == 1))
+            store(EARLY, cols)
         log_turned_first = sbuf("log_turned_first", F32, S // 2, tag="e0_%d" % EARLY)
         logs_first = log_half_back(log_turned_first[:], turned[0][:], 0, "first")
         subtract(SCALARS, HALVES[0], logs_first[:], y_sb[SCALARS][:, HALVES[0]])
         store(SCALARS, HALVES[0])
-        y_second = after_early[:, HALVES[0]]
-        nc.scalar.copy(y_second, y_psum[SCALARS][1][:])
-        log_turned_second = sbuf("log_turned_second", F32, S // 2)
+        log_turned_second = sbuf("log_turned_second", F32, S // 2, tag="late_seed_0")
         logs_second = log_half_back(log_turned_second[:], turned[1][:], 2, "second")
-        log_late = sbuf("log_late", tag="e0_%d" % EARLY)
-        for cols in HALVES:
+        log_late = sbuf("log_late", tag="e0_copy_%d" % EARLY)
+
+        def finish_late(cols):
             nc.scalar.activation(log_late[:, cols], sum_late[:, cols], LN)
-        subtract(LATE, HALVES[0], log_late[:, HALVES[0]], y_psum[LATE][0][:, HALVES[0]])
-        store(LATE, HALVES[0])
+            subtract(LATE, cols, log_late[:, cols], y_psum[LATE][0][:, cols])
+            store(LATE, cols)
+
+        finish_late(HALVES[0])
         subtract(SCALARS, HALVES[1], logs_second[:], y_second)
         store(SCALARS, HALVES[1])
-        subtract(LATE, HALVES[1], log_late[:, HALVES[1]], y_psum[LATE][0][:, HALVES[1]])
-        store(LATE, HALVES[1])
+        for cols in LAST_QUARTERS:
+            finish_late(cols)

@@ -224,16 +224,16 @@ def tile_picked_nce8_none_p_kernel(tc, x_words, x_scales, w1, offs, n1, n2, n3, 
                     nc.tensor.matmul(turned[h][:, P * b : P * (b + 1)], block, identity[:], is_transpose=True, start=(n == 0 and b == 0), stop=(n == 3 and b == 1))
 
         log_early = sbuf("log_early")
-        nc.scalar.activation(log_early[:], sum_early[:], LN)
+        logs_scalars = []
+        for h, cols in enumerate(HALVES):
+            nc.scalar.activation(log_early[:, cols], sum_early[:, cols], LN)
+            log_turned = sbuf("log_turned_scalars_%d" % h, F32, S // 2, tag=("e0_%d" % EARLY, "late_seed_0")[h])
+            logs_scalars.append(log_half_back(log_turned[:], turned[h][:], (0, 2)[h], "scalars_%d" % h))
         for h, cols in enumerate(HALVES):
             subtract(EARLY, cols, log_early[:, cols], y_psum[EARLY][h][:])
             store(EARLY, cols)
-        log_turned_first = sbuf("log_turned_first", F32, S // 2, tag="e0_%d" % EARLY)
-        logs_first = log_half_back(log_turned_first[:], turned[0][:], 0, "first")
-        subtract(SCALARS, HALVES[0], logs_first[:], y_sb[SCALARS][:, HALVES[0]])
+        subtract(SCALARS, HALVES[0], logs_scalars[0][:], y_sb[SCALARS][:, HALVES[0]])
         store(SCALARS, HALVES[0])
-        log_turned_second = sbuf("log_turned_second", F32, S // 2, tag="late_seed_0")
-        logs_second = log_half_back(log_turned_second[:], turned[1][:], 2, "second")
         log_late = sbuf("log_late", tag="e0_copy_%d" % EARLY)
 
         def finish_late(cols):
@@ -242,7 +242,7 @@ def tile_picked_nce8_none_p_kernel(tc, x_words, x_scales, w1, offs, n1, n2, n3, 
             store(LATE, cols)
 
         finish_late(HALVES[0])
-        subtract(SCALARS, HALVES[1], logs_second[:], y_second)
+        subtract(SCALARS, HALVES[1], logs_scalars[1][:], y_second)
         store(SCALARS, HALVES[1])
         for cols in LAST_QUARTERS:
             finish_late(cols)

@@ -181,10 +181,11 @@ def tile_picked_nce8_none_p_kernel(tc, x_words, x_scales, w1, offs, n1, n2, n3, 
         nc.scalar.activation(late_seeds[1][:], y_psum[LATE][0][:, HALVES[1]], EXP)
         nc.sync.dma_start(e0[LATE][:, HALVES[1]], late_seeds[1][:])
         shared_n1 = scalar_lookup(SHARED, 0, [WHOLE], sbuf("shared_n1"))
-        scalar_lookup(SHARED, 1, HALVES[1:], shared_n2)
-        turned_shared = turned_sum([e0[SHARED], shared_n3, shared_n1, shared_n2], 7, "turned_shared", S)
         for h in (1, 0):
             nc.scalar.activation(e0[SCALARS][:, HALVES[h]], y_psum[SCALARS][h][:], EXP)
+        scalar_lookup(SHARED, 1, HALVES[1:], shared_n2)
+        turned_shared = turned_sum([e0[SHARED], shared_n3, shared_n1, shared_n2], 7, "turned_shared", S)
+        nc.vector.tensor_copy(y_sb[SCALARS][:, HALVES[1]], y_psum[SCALARS][1][:])
 
         sum_early = lookup_and_add(EARLY, 0, e0_copy[EARLY], HALVES, sbuf("sum_early_0"))
         sum_late = sbuf("sum_late_0")
@@ -202,9 +203,8 @@ def tile_picked_nce8_none_p_kernel(tc, x_words, x_scales, w1, offs, n1, n2, n3, 
         late_middle = sbuf("sum_late_1")
         lookup_and_add(LATE, 1, sum_late, HALVES[:1], late_middle)
         log_turned_shared = sbuf("log_turned_shared")
-        after_seed = sbuf("after_seed", F32, S + S // 2, tag="late_seed_1")
-        loss[SHARED], y_second = after_seed[:, :S], after_seed[:, S:]
-        nc.vector.tensor_copy(y_second[:, :P], y_psum[SCALARS][1][:, :P])
+        after_seed = sbuf("after_seed", F32, 4 * S, tag="late_seed_1")
+        loss[SHARED], found = after_seed[:, :S], after_seed[:, S:]
         for h, cols in enumerate(HALVES):
             logs = log_half_back(log_turned_shared[:, cols], turned_shared[:, cols], (0, 2)[h], "shared_%d" % h)
             subtract(SHARED, cols, logs[:], y_sb[SHARED][:, cols])
@@ -213,8 +213,6 @@ def tile_picked_nce8_none_p_kernel(tc, x_words, x_scales, w1, offs, n1, n2, n3, 
         lookup_and_add(LATE, 1, sum_late, HALVES[1:], late_middle)
         sum_late = lookup_and_add(LATE, 2, late_middle, HALVES, sbuf("sum_late_2"))
 
-        nc.scalar.copy(y_second[:, P:], y_psum[SCALARS][1][:, P:])
-        found = sbuf("found_scalars", F32, 3 * S, tag="e0_copy_%d" % EARLY)
         terms = [e0[SCALARS]] + [scalar_lookup(SCALARS, i, [WHOLE] if i < 2 else HALVES, found[:, S * i : S * (i + 1)]) for i in range(3)]
         turned = [bank(3, "turned_first", S // 2), bank(7, "turned_second", S // 2)]
         for n, term in enumerate(terms):
@@ -234,7 +232,7 @@ def tile_picked_nce8_none_p_kernel(tc, x_words, x_scales, w1, offs, n1, n2, n3, 
             store(EARLY, cols)
         subtract(SCALARS, HALVES[0], logs_scalars[0][:], y_sb[SCALARS][:, HALVES[0]])
         store(SCALARS, HALVES[0])
-        log_late = sbuf("log_late", tag="e0_copy_%d" % EARLY)
+        log_late = sbuf("log_late", tag="late_seed_1")
 
         def finish_late(cols):
             nc.scalar.activation(log_late[:, cols], sum_late[:, cols], LN)
@@ -242,7 +240,7 @@ def tile_picked_nce8_none_p_kernel(tc, x_words, x_scales, w1, offs, n1, n2, n3, 
             store(LATE, cols)
 
         finish_late(HALVES[0])
-        subtract(SCALARS, HALVES[1], logs_scalars[1][:], y_second)
+        subtract(SCALARS, HALVES[1], logs_scalars[1][:], y_sb[SCALARS][:, HALVES[1]])
         store(SCALARS, HALVES[1])
         for cols in LAST_QUARTERS:
             finish_late(cols)

@@ -203,8 +203,8 @@ def tile_picked_nce8_none_p_kernel(tc, x_words, x_scales, w1, offs, n1, n2, n3, 
         late_middle = sbuf("sum_late_1")
         lookup_and_add(LATE, 1, sum_late, HALVES[:1], late_middle)
         log_turned_shared = sbuf("log_turned_shared")
-        after_seed = sbuf("after_seed", F32, 4 * S, tag="late_seed_1")
-        loss[SHARED], found = after_seed[:, :S], after_seed[:, S:]
+        loss[SHARED] = sbuf("loss_shared", tag="late_seed_1")
+        found = sbuf("found_scalars", F32, 3 * S, tag="picked_words")
         for h, cols in enumerate(HALVES):
             logs = log_half_back(log_turned_shared[:, cols], turned_shared[:, cols], (0, 2)[h], "shared_%d" % h)
             subtract(SHARED, cols, logs[:], y_sb[SHARED][:, cols])
@@ -232,7 +232,7 @@ def tile_picked_nce8_none_p_kernel(tc, x_words, x_scales, w1, offs, n1, n2, n3, 
             store(EARLY, cols)
         subtract(SCALARS, HALVES[0], logs_scalars[0][:], y_sb[SCALARS][:, HALVES[0]])
         store(SCALARS, HALVES[0])
-        log_late = sbuf("log_late", tag="late_seed_1")
+        log_late = sbuf("log_late", tag="picked_words")
 
         def finish_late(cols):
             nc.scalar.activation(log_late[:, cols], sum_late[:, cols], LN)

@@ -242,5 +242,4 @@ def tile_picked_nce8_none_p_kernel(tc, x_words, x_scales, w1, offs, n1, n2, n3, 
         finish_late(HALVES[0])
         subtract(SCALARS, HALVES[1], logs_scalars[1][:], y_sb[SCALARS][:, HALVES[1]])
         store(SCALARS, HALVES[1])
-        for cols in LAST_QUARTERS:
-            finish_late(cols)
+        finish_late(HALVES[1])

from contextlib import ExitStack

import concourse.mybir as mybir
from concourse.masks import make_identity

K, T, S, N = 512, 2048, 512, 512
FLOPS = 2 * K * N * S

F32 = mybir.dt.float32
BF16 = mybir.dt.bfloat16
I32 = mybir.dt.int32
U32 = mybir.dt.uint32
U16 = mybir.dt.uint16
U8 = mybir.dt.uint8
FP8X4 = mybir.dt.float8_e4m3fn_x4
COPY = mybir.ActivationFunctionType.Copy
EXP = mybir.ActivationFunctionType.Exp
LN = mybir.ActivationFunctionType.Ln
ADD = mybir.AluOpType.add
SUB = mybir.AluOpType.subtract

P = 128
PACK = 4
TILES = N // P
PER_LIST_COLUMN = 16
SHARED, EARLY, LATE, SCALARS = 0, 1, 2, 3

WHOLE = slice(0, S)
HALVES = [slice(0, S // 2), slice(S // 2, S)]
LAST_QUARTERS = [slice(S // 2, S // 2 + P), slice(S // 2 + P, S)]
WINDOW = 2 * S
VECTOR_ROWS = 92
W_LOADS = [slice(0, 2), slice(2, PACK)]


def tile_picked_nce8_none_p_kernel(tc, x_words, x_scales, w1, offs, n1, n2, n3, out):
    nc = tc.nc
    with ExitStack() as ctx:
        keep = ctx.enter_context(tc.tile_pool(name="keep", bufs=1))
        psum = ctx.enter_context(tc.psum_pool(name="psum", bufs=1))

        def sbuf(name, dtype=F32, width=S, tag=None):
            return keep.tile([P, width], dtype, name=name, tag=tag or name, align_bytes=64)

        def bank(number, name, width):
            return psum.tile([P, width], F32, name=name, tag="bank%d" % number)

        def entries(list_tile, cols):
            return list_tile[:, cols.start // PER_LIST_COLUMN : cols.stop // PER_LIST_COLUMN]

        key_scales = sbuf("key_scales", U8, T)
        nc.vector.memset(key_scales[:].bitcast(I32), 0)

        w_raw = keep.tile([P, PACK, N], F32, name="w_raw")
        w_rows = w1.rearrange("(p r) c -> p r c", r=PACK)
        nc.sync.dma_start(w_raw[:, W_LOADS[0], :], w_rows[:, W_LOADS[0], :])
        offs_sb = keep.tile([P, S // PER_LIST_COLUMN], U16, name="offs_sb")
        nc.sync.dma_start(offs_sb[:], offs)
        nc.sync.dma_start(key_scales[0:P:8, :].bitcast(I32), x_scales[0].bitcast(I32))
        nc.sync.dma_start(w_raw[:, W_LOADS[1], :], w_rows[:, W_LOADS[1], :])
        key_words = sbuf("key_words", U32, T)
        nc.sync.dma_start(key_words[:].bitcast(I32), x_words[0].rearrange("p c r -> p (c r)").bitcast(I32))
        negatives = []
        for name, source in (("n1_sb", n1), ("n2_sb", n2), ("n3_sb", n3)):
            list_sb = keep.tile([P, S // PER_LIST_COLUMN], U16, name=name)
            nc.sync.dma_start(list_sb[:], source)
            negatives.append(list_sb)

        identity = sbuf("identity", F32, P)
        make_identity(nc, identity[:])

        spread_scales = sbuf("spread_scales", U8)
        nc.vector.tensor_copy(spread_scales[:], key_scales[:].indirect(offs_sb[:]))
        picked_scales = sbuf("picked_scales", U8)
        nc.vector.memset(picked_scales[:].bitcast(I32), 0)
        for q in range(4):
            nc.scalar.dma_start(picked_scales[32 * q : 32 * q + 4, :].bitcast(I32), spread_scales[32 * q : 32 * q + 32 : 8, :].bitcast(I32))

        w_grouped = sbuf("w_grouped", BF16, PACK * N)
        grouped_view = w_grouped[:].rearrange("p (t m r) -> p m r t", t=TILES, r=PACK)
        raw_view = w_raw[:].rearrange("p r (m t) -> p m r t", t=TILES)
        nc.vector.tensor_copy(grouped_view[:, :, :, :2], raw_view[:, :, :, :2])
        for planes in W_LOADS:
            nc.scalar.activation(grouped_view[:, :, planes, 2:], raw_view[:, :, planes, 2:], COPY)
        w_scales = sbuf("w_scales", U8, N)

        def quantise_pair(pair, tag):
            codes = sbuf("w_codes_%d" % pair, U32, N // 2, tag=tag)
            cols = slice(pair * N // 2, (pair + 1) * N // 2)
            nc.vector.quantize_mx(out=codes[:].bitcast(FP8X4), scales=w_scales[:, cols], in_=w_grouped[:, PACK * cols.start : PACK * cols.stop])
            return codes

        w_codes = [quantise_pair(0, None)]

        picked_words = sbuf("picked_words", U32)
        for cols in HALVES:
            nc.vector.tensor_copy(picked_words[:, cols], key_words[:].indirect(entries(offs_sb, cols)))
        w_codes.append(quantise_pair(1, "key_words"))

        y_psum = {t: [] for t in range(TILES)}

        def product(t, cols, number):
            scores = bank(number, "y_%d_from_%d" % (t, cols.start), cols.stop - cols.start)
            nc.tensor.matmul_mx(
                out=scores[:],
                lhsT=w_codes[t // 2][:, P * (t % 2) : P * (t % 2 + 1)].bitcast(FP8X4),
                lhsT_scale=w_scales[:, P * t : P * (t + 1)],
                rhs=picked_words[:, cols].bitcast(FP8X4),
                rhs_scale=picked_scales[:, cols],
                start=True,
                stop=True,
            )
            y_psum[t].append(scores)

        product(SHARED, HALVES[0], 0)
        product(EARLY, HALVES[0], 1)
        product(SHARED, LAST_QUARTERS[0], 2)
        product(SHARED, LAST_QUARTERS[1], 3)
        product(EARLY, HALVES[1], 4)
        product(LATE, WHOLE, 5)

        e0 = [sbuf("e0_%d" % t, F32, WINDOW) for t in range(TILES)]
        y_sb = {t: sbuf("y_%d" % t) for t in (SHARED, SCALARS)}
        e0_copy = {EARLY: sbuf("e0_copy_%d" % EARLY)}
        late_seeds = [sbuf("late_seed_%d" % h, F32, S // 2) for h in range(2)]

        def shared_piece(piece, cols):
            nc.scalar.activation(e0[SHARED][:, cols], y_psum[SHARED][piece][:], EXP)
            nc.vector.tensor_copy(y_sb[SHARED][:, cols], y_psum[SHARED][piece][:])

        shared_piece(0, HALVES[0])
        nc.scalar.activation(e0[EARLY][:, HALVES[0]], y_psum[EARLY][0][:], EXP)
        nc.vector.tensor_copy(e0_copy[EARLY][:, HALVES[0]], e0[EARLY][:, HALVES[0]])
        shared_piece(1, LAST_QUARTERS[0])
        nc.scalar.activation(e0[SHARED][:, LAST_QUARTERS[1]], y_psum[SHARED][2][:], EXP)
        nc.scalar.activation(e0[EARLY][:, HALVES[1]], y_psum[EARLY][1][:], EXP)
        nc.sync.dma_start(e0_copy[EARLY][:, HALVES[1]], e0[EARLY][:, HALVES[1]])
        nc.scalar.copy(y_sb[SHARED][:, LAST_QUARTERS[1]], y_psum[SHARED][2][:])
        product(SCALARS, HALVES[0], 3)
        product(SCALARS, HALVES[1], 6)

        def scalar_lookup(t, i, spans, found):
            for cols in spans:
                nc.scalar.activation(found[:, cols], e0[t][:].indirect(entries(negatives[i], cols)), COPY)
            return found

        def vector_lookup(t, i, tag=None):
            found = sbuf("found_%d_%d" % (t, i), tag=tag)
            nc.vector.tensor_copy(found[:], e0[t][:].indirect(negatives[i][:]))
            return found

        def lookup_and_add(t, i, total, spans, grown):
            for cols in spans:
                nc.vector.tensor_tensor(grown[:, cols], e0[t][:].indirect(entries(negatives[i], cols)), total[:, cols], ADD)
            return grown

        def turned_sum(terms, number, name, width):
            turned = bank(number, name, width)
            blocks = width // P
            for n, term in enumerate(terms):
                for b in range(blocks):
                    cols = slice(P * b, P * (b + 1))
                    nc.tensor.matmul(turned[:, cols], term[:, cols], identity[:], is_transpose=True, start=(n == 0 and b == 0), stop=(n == len(terms) - 1 and b == blocks - 1))
            return turned

        out_rows = out.rearrange("(p t) j -> p t j", t=TILES)
        loss = {t: sbuf("loss_%d" % t) for t in (EARLY, LATE, SCALARS)}

        def subtract(t, cols, logs, scores):
            nc.vector.tensor_tensor(loss[t][:, cols], logs, scores, SUB)

        def store(t, cols):
            nc.sync.dma_start(out_rows[:, t, cols], loss[t][:, cols])

        shared_n3 = vector_lookup(SHARED, 2)
        nc.vector.tensor_copy(y_sb[SCALARS][:, HALVES[0]], y_psum[SCALARS][0][:])
        shared_n2 = sbuf("shared_n2", tag="picked_words")
        nc.vector.tensor_copy(shared_n2[:, HALVES[0]], e0[SHARED][:].indirect(entries(negatives[1], HALVES[0])))
        nc.scalar.activation(e0[LATE][:, HALVES[0]], y_psum[LATE][0][:, HALVES[0]], EXP)
        nc.sync.dma_start(late_seeds[0][:], e0[LATE][:, HALVES[0]])
        nc.scalar.activation(late_seeds[1][:], y_psum[LATE][0][:, HALVES[1]], EXP)
        nc.sync.dma_start(e0[LATE][:, HALVES[1]], late_seeds[1][:])
        shared_n1 = scalar_lookup(SHARED, 0, [WHOLE], sbuf("shared_n1"))
        for h in (1, 0):
            nc.scalar.activation(e0[SCALARS][:, HALVES[h]], y_psum[SCALARS][h][:], EXP)
        scalar_lookup(SHARED, 1, HALVES[1:], shared_n2)
        turned_shared = turned_sum([e0[SHARED], shared_n3, shared_n1, shared_n2], 7, "turned_shared", S)
        nc.vector.tensor_copy(y_sb[SCALARS][:, HALVES[1]], y_psum[SCALARS][1][:])

        sum_early = lookup_and_add(EARLY, 0, e0_copy[EARLY], HALVES, sbuf("sum_early_0"))
        sum_late = sbuf("sum_late_0")
        for h, cols in enumerate(HALVES):
            nc.vector.tensor_tensor(sum_late[:, cols], e0[LATE][:].indirect(entries(negatives[0], cols)), late_seeds[h][:], ADD)
        sum_early = lookup_and_add(EARLY, 1, sum_early, [WHOLE], sbuf("sum_early_1", tag="late_seed_0"))

        def log_half_back(log_turned, turned, number, name):
            nc.scalar.activation(log_turned, turned, LN)
            logs = bank(number, "logs_" + name, S // 2)
            for b in range(2):
                nc.tensor.transpose(logs[:, P * b : P * (b + 1)], log_turned[:, P * b : P * (b + 1)], identity[:])
            return logs

        late_middle = sbuf("sum_late_1")
        lookup_and_add(LATE, 1, sum_late, HALVES[:1], late_middle)
        log_turned_shared = sbuf("log_turned_shared")
        loss[SHARED] = sbuf("loss_shared", tag="late_seed_1")
        found = sbuf("found_scalars", F32, 3 * S, tag="picked_words")
        for h, cols in enumerate(HALVES):
            logs = log_half_back(log_turned_shared[:, cols], turned_shared[:, cols], (0, 2)[h], "shared_%d" % h)
            subtract(SHARED, cols, logs[:], y_sb[SHARED][:, cols])
        store(SHARED, WHOLE)
        sum_early = lookup_and_add(EARLY, 2, sum_early, [WHOLE], sbuf("sum_early_2"))
        lookup_and_add(LATE, 1, sum_late, HALVES[1:], late_middle)
        sum_late = lookup_and_add(LATE, 2, late_middle, HALVES, sbuf("sum_late_2"))

        terms = [e0[SCALARS]] + [scalar_lookup(SCALARS, i, [WHOLE] if i < 2 else HALVES, found[:, S * i : S * (i + 1)]) for i in range(3)]
        turned = [bank(3, "turned_first", S // 2), bank(7, "turned_second", S // 2)]
        for n, term in enumerate(terms):
            for h, cols in enumerate(HALVES):
                for b in range(2):
                    block = term[:, cols.start + P * b : cols.start + P * (b + 1)]
                    nc.tensor.matmul(turned[h][:, P * b : P * (b + 1)], block, identity[:], is_transpose=True, start=(n == 0 and b == 0), stop=(n == 3 and b == 1))

        log_early = sbuf("log_early")
        logs_scalars = []
        for h, cols in enumerate(HALVES):
            nc.scalar.activation(log_early[:, cols], sum_early[:, cols], LN)
            log_turned = sbuf("log_turned_scalars_%d" % h, F32, S // 2, tag=("e0_%d" % EARLY, "late_seed_0")[h])
            logs_scalars.append(log_half_back(log_turned[:], turned[h][:], (0, 2)[h], "scalars_%d" % h))
        for h, cols in enumerate(HALVES):
            subtract(EARLY, cols, log_early[:, cols], y_psum[EARLY][h][:])
            store(EARLY, cols)
        subtract(SCALARS, HALVES[0], logs_scalars[0][:], y_sb[SCALARS][:, HALVES[0]])
        store(SCALARS, HALVES[0])
        log_late = sbuf("log_late", tag="picked_words")

        def finish_late(cols):
            nc.scalar.activation(log_late[:, cols], sum_late[:, cols], LN)
            subtract(LATE, cols, log_late[:, cols], y_psum[LATE][0][:, cols])
            store(LATE, cols)

        finish_late(HALVES[0])
        subtract(SCALARS, HALVES[1], logs_scalars[1][:], y_sb[SCALARS][:, HALVES[1]])
        store(SCALARS, HALVES[1])
        finish_late(HALVES[1])
